import numpy as np, ml_dtypes
CORES = [35,38,43,46]
N = 4
import mx_ref
BF = ml_dtypes.bfloat16
def entries(a):
    return np.ascontiguousarray(a.T).reshape(-1)
def table(e):
    return np.ascontiguousarray(np.reshape(e, (-1, 16)).T).astype(np.int32)
def pick(q, e):
    c = np.concatenate([q[0].reshape(128, -1, 4), np.zeros((128, 1, 4), np.uint8)], axis=1); s = np.concatenate([q[1], np.ones((16, 1), np.uint8)], axis=1)
    return (np.ascontiguousarray(c[:, e].reshape(128, -1)), np.ascontiguousarray(s[:, e]))
def join(*qs):
    return (np.concatenate([q[0] for q in qs], axis=1), np.concatenate([q[1] for q in qs], axis=1))
def put(q, e, v):
    c, s = q[0].reshape(128, -1, 4).copy(), q[1].copy(); c[:, e] = v[0].reshape(128, -1, 4); s[:, e] = v[1]
    return (c.reshape(128, -1), s)
def pk(c, s):
    return (np.ascontiguousarray(c), mx_ref.live(s))
def emit(q):
    return q[0], q[1]
def cut(t, i, w=512):
    return t[:, w * i:w * i + w]
def f(rng, *shape):
    return mx_ref.flush((rng.standard_normal(shape, dtype=np.float32) * np.exp2(rng.integers(-2, 3, shape[:-1] + (1,)))).astype(BF))
def wide(rng, *shape, cols=0):
    v = rng.standard_normal(shape, dtype=np.float32) * np.exp2(rng.integers(-12, 13, shape)).astype(np.float32)
    if cols: v *= np.repeat(np.exp2(rng.integers(-cols, cols + 1, shape[:-2] + (1, shape[-1] // 4))) * (rng.random(shape[:-2] + (1, shape[-1] // 4)) > 0.0625), 4, axis=-1).astype(np.float32)
    return mx_ref.flush(v.astype(BF))
P, K, R, LC = 256, 48, 3, 96
def near(nb):
    return np.stack([entries(nb[r]).reshape(P, 3) for r in range(N)]).astype(np.int64)
def play(x, bb, nb, u, v, a):
    n = near(nb)
    X = join(*[mx_ref.quantize(np.ascontiguousarray(x[r])) for r in range(N)])
    qu, qv = mx_ref.quantize(np.ascontiguousarray(u[0])), mx_ref.quantize(np.ascontiguousarray(v[0]))
    qa = [[mx_ref.quantize(np.ascontiguousarray(cut(a[r], i))) for i in range(4)] for r in range(N)]
    fixed = [mx_ref.matmul(qv, mx_ref.quantize(np.ascontiguousarray(bb[r])))[0] for r in range(N)]
    b = bb.astype(np.float32).reshape(N, 128, P, 4)
    done, res, made = np.zeros((N, R, K), np.int64), [], []
    for t in range(R):
        e = mx_ref.matmul(qu, X)[0]
        new = []
        for r in range(N):
            z = ((e[n[r, :, 0]] + e[n[r, :, 1]]) + e[n[r, :, 2]]) - fixed[r]
            j = np.argsort(-np.abs(z), kind="stable")[:K]
            nbs = pick(X, n[r, j].T.reshape(-1))
            s = []
            for i in range(4):
                m = mx_ref.matmul(qa[r][i], nbs)
                s.append((m[:, :K] + m[:, K:2 * K]) + m[:, 2 * K:])
            g = np.float32(0.05) * np.stack(s, axis=2) + b[r][:, j]
            new.append(mx_ref.quantize(np.ascontiguousarray(g.reshape(128, -1).astype(BF))))
            done[r, t] = j
            res.append(z)
            made.append(g)
        X = put(X, np.concatenate([P * r + done[r, t] for r in range(N)]), join(*new))
    return X, done, np.stack(res), np.stack(made)
def fit(z, g):
    top = np.abs(g.astype(BF).astype(np.float32)).reshape(-1, 16, 8, K, 4).max(axis=(2, 4))
    g = np.abs(g)
    return bool(np.isfinite(z).all() and np.isfinite(g).all() and ((g == 0) | (g >= 2.0 ** -60) & (g <= 2.0 ** 60)).all() and ((top == 0) | (top >= 2.0 ** -30) & (top <= 2.0 ** 30)).all())
def bf(v):
    return mx_ref.flush(np.asarray(v, np.float32).astype(BF))
def lone(c):
    t = np.zeros((N, 128, 512), BF)
    t[:, :, :4] = c
    return t
def few(rng, q, n, free, most):
    p = rng.permutation(free)[:most]
    return q * P + rng.permutation(np.concatenate([p, p[rng.integers(0, p.size, P)]])[:n])
def graph(rng, src=None, free=None, most=LC):
    n = np.zeros((N, P, 3), np.int64)
    if free is None: free = [np.arange(P)] * N
    for r in range(N):
        n[r, :, :2] = r * P + rng.choice(free[r], (P, 2))
        s = (r + rng.integers(1, N, P)) % N if src is None else np.full(P, src[r])
        for q in range(N):
            i = np.flatnonzero(s == q)
            n[r, i, 2] = few(rng, q, i.size, free[q], most)
    return n
def stored(n):
    return np.stack([table(n[r].reshape(-1)) for r in range(N)])
def setup_inputs(rng):
    return {"x": f(rng, N, 128, 4 * P), "bb": f(rng, N, 128, 4 * P), "nb": stored(graph(rng)), "u": lone(f(rng, 128, 4)), "v": lone(f(rng, 128, 4)),
            "a": bf(f(rng, N, 128, 2048).astype(np.float32) * np.float32(2.0 ** -4)), "w": f(rng, N, 128, 512)}
def signs(rng):
    return 1.0 - 2.0 * rng.integers(0, 2, (128, 4))
def signed(rng, sg, size):
    return bf(((1 + rng.random((N, 128, P, 4))) * size[:, None, :, None] * sg[:, None, :] + 0.0).reshape(N, 128, 4 * P))
def single(rng, sg, size):
    return lone(bf((1 + rng.random((128, 4))) * sg * size))
def setup_inputs_again(rng):
    d, sg, size, m = setup_inputs(rng), signs(rng), np.zeros((N, P)), K // 8
    o = np.stack([rng.permutation(P) for r in range(N)])
    rest = np.sort(o[:, 7 * m:], axis=1)
    hold = np.stack([rng.permutation(rest[r, -5:]) for r in range(N)])
    n = graph(rng, free=rest[:, :-5], most=LC - 2)
    large, small = (1 + rng.random((128, 4))) * sg * 2.0 ** 20, (1 + rng.random((128, 4))) * sg * 2.0 ** -8
    top = np.arange(128)[:, None] < 64
    five = np.stack([large * top, large * ~top, -large, large, small], axis=1) + 0.0
    x = np.zeros((N, 128, P, 4))
    for r in range(N):
        x[r][:, hold[r]] = five
        h, left, both, alone = o[r, :4 * m], o[r, 4 * m:5 * m], o[r, 5 * m:6 * m], o[r, 6 * m:7 * m]
        size[r, h] = 64
        size[r, left] = 64
        n[r, h, 0] = r * P + rng.permutation(h)
        n[r, left, 0], n[r, left, 1] = r * P + hold[r, 0], r * P + hold[r, 1]
        n[r, both, 0], n[r, both, 1] = r * P + hold[r, 3], r * P + hold[r, 2]
        for i, k in ((left, 2), (both, 4), (alone, 4)):
            q = n[r, i, 2] // P
            n[r, i, 2] = q * P + hold[q, k]
    bb = signed(rng, sg, size).reshape(N, 128, P, 4)
    for r in range(N): bb[r][8:, o[r, 4 * m:5 * m]] = 0
    d.update(x=bf(x.reshape(N, 128, 4 * P)), bb=bb.reshape(N, 128, 4 * P), nb=stored(n), u=single(rng, sg, 1.0), v=single(rng, sg, 4.0))
    return d
def setup_inputs_far(rng):
    h = int(rng.integers(0, N))
    src = np.full(N, h)
    src[h] = (h + int(rng.integers(1, N))) % N
    d, n, sg, size = setup_inputs(rng), graph(rng, src), signs(rng), np.full((N, P), 2.0 ** 20)
    for r in range(N):
        first = np.unique(n[r, :, 2], return_index=True)[1]
        size[r, rng.permutation(first)[:K]] = 2.0 ** 26
    d.update(x=signed(rng, sg, np.full((N, P), 2.0 ** 20)), bb=signed(rng, sg, size), nb=stored(n), u=single(rng, sg, 2.0 ** 23), v=single(rng, sg, 2.0 ** 29))
    return d
def setup_inputs_moved(rng):
    d, n, sg, size = setup_inputs(rng), np.zeros((N, P, 3), np.int64), signs(rng), np.full((N, P), 2.0 ** -4)
    o = [rng.permutation(P) for r in range(N)]
    for r in range(N):
        size[r, o[r][:K]] = 64
        n[r, :, :2] = r * P + rng.choice(o[r][K:], (P, 2))
        m = np.zeros(P, bool)
        m[rng.permutation(P)[:K + K // 2]] = True
        s = (r + rng.integers(1, N, P)) % N
        for q in range(N):
            hot, cold = rng.permutation(o[q][:K])[:LC // 2], rng.permutation(o[q][K:])[:LC - LC // 2]
            i, k = np.flatnonzero((s == q) & m), np.flatnonzero((s == q) & ~m)
            n[r, i, 2] = q * P + rng.choice(hot, i.size)
            n[r, k, 2] = q * P + rng.choice(cold, k.size)
    d.update(x=signed(rng, sg, np.full((N, P), 2.0 ** -6)), bb=signed(rng, sg, size), nb=stored(n), u=single(rng, sg, 16.0), v=single(rng, sg, 1.0))
    return d
def setup_inputs_spread(rng):
    d = setup_inputs(rng)
    d["x"] = wide(rng, N, 128, 4 * P, cols=4)
    d["bb"] = wide(rng, N, 128, 4 * P, cols=4)
    return d
def setup_inputs_ties(rng):
    d, n = setup_inputs(rng), np.zeros((N, P, 3), np.int64)
    kind = np.stack([rng.permutation(np.arange(P) % 4) for r in range(N)])
    for k in ("x", "bb"):
        c = f(rng, 128, 8).astype(np.float32).reshape(128, 2, 4)
        d[k] = np.stack([bf((c[:, kind[r] >> 1] * (1 - 2 * (kind[r] & 1))[None, :, None]).reshape(128, -1)) for r in range(N)])
    for r in range(N):
        s = (r + rng.integers(1, N, P)) % N
        for k in range(4):
            i = np.flatnonzero(kind[r] == k)
            n[r, i, 0] = r * P + rng.choice(i, i.size)
            n[r, i, 1] = r * P + rng.choice(np.flatnonzero(kind[r] == (k ^ 2)), i.size)
            for q in range(N):
                j = i[s[i] == q]
                n[r, j, 2] = q * P + rng.choice(rng.permutation(np.flatnonzero(kind[q] == k))[:LC // 4], j.size)
    d["nb"] = stored(n)
    return d
def check_inputs(d):
    b = []
    for k in ("x", "bb", "u", "v", "a", "w"):
        t = np.abs(d[k].astype(np.float32))
        if not (np.isfinite(t).all() and ((t == 0) | (t >= 2.0 ** -30) & (t <= 2.0 ** 30)).all()): b.append("a value of " + k)
    for k in ("u", "v"):
        t = d[k].astype(np.float32)
        if (t[:, :, 4:] != 0).any(): b.append(k + " has numbers behind its column 0")
        if (t != t[:1]).any(): b.append(k + " isn't the same on all ranks")
    n = near(d["nb"])
    at, own = n // P, np.arange(N)[:, None, None]
    if n.min() < 0 or n.max() >= N * P or (at[:, :, :2] != own).any() or (at[:, :, 2] == own[:, :, 0]).any(): b.append("nb")
    elif any(np.unique(n[r, :, 2][at[r, :, 2] == q]).size > LC for r in range(N) for q in range(N)): b.append("nb names too many columns of one rank")
    if not b:
        try:
            with np.errstate(all="ignore"):
                X, done, z, g = play(d["x"], d["bb"], d["nb"], d["u"], d["v"], d["a"])
                good = fit(z, g)
        except Exception:
            good = False
        if not good: b.append("a number that the rounds make")
    return b
def reference(x, bb, nb, u, v, a, w):
    X, done, z, g = play(x, bb, nb, u, v, a)
    oc, osc, y = np.zeros((N, 128, 4 * P), np.uint8), np.zeros((N, 16, P), np.uint8), np.zeros((N, 128, P), np.float32)
    for r in range(N):
        q = pick(X, np.arange(P * r, P * r + P))
        oc[r], osc[r] = emit(q)
        y[r] = mx_ref.matmul(mx_ref.quantize(np.ascontiguousarray(w[r])), q)
    return {"oc": oc, "osc": osc, "nd": done.astype(np.float32), "y": y}

@@ -1,0 +1,615 @@
+from concourse.bass import DstId, RemoteDMATransfer
+from concourse.mybir import AluOpType as OP, AxisListType, ActivationFunctionType as AF, dt
+
+P, K, R, LC = 256, 48, 3, 96
+OWN = [P, P + K]
+FAR = P + K + 128
+ARR = [FAR + 3 * LC, FAR + 3 * LC + 3 * K]
+OWN.append(ARR[1] + 3 * K)
+WEND = [ARR[0], ARR[1], OWN[2]]
+WC = OWN[2] + 128
+PW = 2 * K + 128
+TINY = 2.0 ** -122
+PRED = 1.0 - 2.0 ** -24
+STEP, MID = 2.0 ** 19, 2.0 ** 24
+STEP1 = 512.0
+UP = 2.0 ** 23
+VPART = 128
+NP = 2
+INP = 2
+SCN_S = 2
+LEN_S = 3
+ORDER = [int(_i) for _i in """
+53 10 8 23 48 11 9 0 6 4 24 1 5 2 37 3 7 34 12 13 47 14 15 38 16 36 17 18 41 39 19 25 189 46 20 21 30 31 26 22 32 67 57 60 27 74 61 62 73 68 188 33 85 69 63 86 64 58 143 83 84 146 65 66 182 75 77 28 78 185 144 59 105 163 195 108 70 87 106 79 90 93 80 81 88 96 91 109 99 102 107 94 89 97 92 100 110 95 103 98 145 101 54 104 55 56 35 111 148 150 112 82 42 129 126 127 113 128 147 115 119 117 114 116 120 154 118 149 121 122 71 123 72 124 157 155 167 162 156 76 151 130 159 158 164 212 173 160 131 132 133 213 134 135 161 136 168 137 45 169 138 170 139 214 171 140 141 29 50 222 165 166 125 223 153 215 216 200 224 201 172 203 202 225 226 142 240 40 227 205 207 204 238 229 230 231 206 232 234 233 235 236 217 228 237 239 241 194 219 242 218 243 198 220 244 221 49 246 174 247 245 248 250 196 249 175 251 177 252 254 208 253 178 303 255 197 256 259 257 258 260 152 261 199 262 263 264 266 304 265 43 267 268 269 176 270 279 272 271 281 179 273 282 280 289 283 284 285 286 180 275 274 183 294 181 52 184 290 44 295 291 276 296 292 278 297 287 51 293 288 298 299 301 300 302 314 355 191 305 306 309 307 209 359 277 336 187 315 210 356 357 358 325 326 310 311 192 337 186 190 312 340 338 316 339 317 341 308 318 319 320 327 193 360 313 362 329 330 331 322 363 328 321 211 323 364 324 342 344 365 343 366 370 333 371 367 372 332 377 373 374 375 334 378 376 369 380 379 368 381 382 383 385 384 345 346 386 388 387 390 389 347 392 391 393 395 397 394 348 396 351 398 349 399 400 352 401 403 404 402 353 405 406 411 412 407 410 335 350 408 469 361 470 471 415 413 414 472 354 416 417 428 418 419 439 429 420 423 477 421 473 440 409 424 450 478 474 430 451 425 431 433 432 434 426 441 422 452 454 480 427 435 443 475 453 481 442 482 479 483 455 444 437 436 445 476 438 484 488 489 446 485 490 496 495 487 491 448 447 493 494 492 498 497 486 500 499 456 501 503 502 457 458 460 504 506 459 508 505 461 510 507 509 511 513 515 462 512 514 465 516 463 449 517 518 466 519 520 464 521 522 524 523 467 525 549 526 550 551 537 536 552 541 527 528 539 538 468 540 529 542 543 530 531 544 553 533 532 534 546 554 535 545 547 548 555 556 559 557 560 558 561 562
+""".split()]
+
+BUF = {
+    "float32": "ID:%d JB:64 Fm:128 Ft:128 FRA:192 FRB:192 FR:192 SLf:256 LJ:768 SJ:256 Mo:256 MoD:512 LRo:512 LRf:256 LIo:64 LIf:32 en:96 G4:192 ST:1024 M:1024 ec:2 EM:768 E1:%d fb:64 PC:192 PAB:128 PAYT:128 PDn:384 PTn:384 PD:384 PT:384 EG:64 zK:64 z0:64 z1:64 z2:64 zr:64 ZT:64 zB:64 zr0:64 Zc:320 KB:192 KEY:192 DK:384 RS:128 nf:9 SU:768 FT:512 ys:256 yn:144" % (WC, OWN[2]),
+    "bfloat16": "ZB:256 xt:1024 bt:1024 at:2048 wt:512 uvs:32 uvt:1024 bbT:1024 EQ:2048 SC:1024 PB:256 PR:256 SCN:256 LE:1536 LC2:768 MK:512 H:512",
+    "int32": "pI:8 ti:24 nbI:12 nbP:24 Ne:28 Ri:6 Di:9 Ji:3 Dj:12",
+    "uint16": "UL:8 DL:32 FN:512 nbG:48 Lu:96 JD:8 KDL:24 nbp:24 nbo:12 nbe:4 nbD:24 nbK:12 FA:256 LST:6 LA:18 LO:18 EO:12 PO:30 J:12 SL0:4 SL1:4 SR0:9 SR1:9 FO:16",
+}
+SMALL = "C12:12 tf:12 GCOL:8 IC:16 ICS:8 TB:4 CK:32 C1:32 PADD:4 LS:8 SS:8 VP:96 PAYJ:4 OFF:192 ZN:4 Rf:4 R0:8 R1:8"
+PART = {}
+_n = 0
+for _b in SMALL.split():
+    PART[_b.split(":")[0]] = _n
+    _n += int(_b.split(":")[1])
+QBUF = "Q0:256 Qb:256 Qa:512 Qw:128 UV2:256 SND:288 W:%d PK0:%d PA1:768 PA2:768 FIN:256" % (WC, PW)
+SCRATCH = {"eld": ("dram", [3, 128, 2], "float32"), "ps": ("psum", [128, 4096], "float32"), "KC": ("sbuf", [128, _n], "float32")}
+for _d, _s in BUF.items():
+    for _b in _s.split():
+        SCRATCH[_b.split(":")[0]] = ("sbuf", [128, int(_b.split(":")[1])], _d)
+for _b in QBUF.split():
+    SCRATCH[_b.split(":")[0]] = ("sbuf", [128, int(_b.split(":")[1])], "float8_e4m3fn_x4")
+    SCRATCH[_b.split(":")[0] + "s"] = ("sbuf", [128, int(_b.split(":")[1])], "uint8")
+SEMAPHORES = "v s p gq d_nb d_nc d_x d_y d_p d_uv d_bb d_a d_w d_q d_m d_e d_nd d_out d_g d_l0 d_l1 d_l2 d_l3 d_l4 d_l5 r_e r_l r_c r_s0 r_s1 r_n0 r_n1 loc".split()
+
+
+def rank_program(g, core, T, topo):
+    rank = T.rank_of(core)
+    if rank is None:
+        return
+    V, S, PE, Y = g.vector, g.scalar, g.tensor, g.sync
+    queue = {"V": V, "S": S, "P": PE, "G": g, "Y": Y}
+    sem_of = {"V": "v", "S": "s", "P": "p", "G": "gq"}
+    count = {s: 0 for s in SEMAPHORES}
+    total = {s: 0 for s in SEMAPHORES}
+    know = {q: {} for q in queue}
+    snaps, touched, calls = {}, {}, []
+
+    def reg(name, c0, c1, p0=0, p1=128, st=1):
+        if name in PART:
+            return ("KC", p0, p1, c0 + PART[name], c1 + PART[name], st)
+        return (name, p0, p1, c0, c1, st)
+
+    def ap(r):
+        n, p0, p1, c0, c1, st = r
+        return T[n][p0:p1, c0:c1:st] if st > 1 else T[n][p0:p1, c0:c1]
+
+    def meet(a, b):
+        if a[0] == "ps":
+            return a[3] // 512 == b[3] // 512
+        if a[2] <= b[1] or b[2] <= a[1] or a[4] <= b[3] or b[4] <= a[3]:
+            return False
+        return not (a[5] == b[5] > 1 and a[3] % a[5] != b[3] % b[5])
+
+    def order(q, reads, writes, acc=False):
+        want = {}
+        for r, w in [(r, False) for r in reads] + [(r, True) for r in writes]:
+            for (o, ow, oq, sem, val) in touched.get(r[0], []):
+                if meet(r, o) and not (acc and oq == q and r[0] == "ps") and (ow or ((w or r[0] == "ps") and oq != q)):
+                    if know[q].get(sem, 0) < val:
+                        want[sem] = max(want.get(sem, 0), val)
+        for s in sorted(want):
+            if any(o != s and snaps.get((o, want[o]), {}).get(s, 0) >= want[s] for o in want):
+                del want[s]
+        for s, val in want.items():
+            queue[q].wait_ge(T.sem[s], val)
+            know[q][s] = max(know[q].get(s, 0), val)
+            for k, x in snaps.get((s, val), {}).items():
+                know[q][k] = max(know[q].get(k, 0), x)
+
+    def note(reads, writes, q, sem, val):
+        for r in reads:
+            touched.setdefault(r[0], []).append((r, False, q, sem, val))
+        for r in writes:
+            touched.setdefault(r[0], []).append((r, True, q, sem, val))
+
+    def op(q, fn, reads, writes, acc=False):
+        s = sem_of[q]
+
+        def emit():
+            order(q, reads, writes, acc)
+            count[s] += 1
+            fn().then_inc(T.sem[s], 1)
+            snaps[(s, count[s])] = dict(know[q])
+            note(reads, writes, q, s, count[s])
+        calls.append(emit)
+
+    def dma(q, sem, out, in_, reads, writes):
+        total[sem] += 16
+
+        def emit():
+            order(q, reads, writes)
+            count[sem] += 16
+            queue[q].dma_start(out, in_).then_inc(T.sem[sem], 16)
+            note(reads, writes, "dma", sem, total[sem])
+        calls.append(emit)
+
+    def arrive(sem, n, *writes):
+        calls.append(lambda: note([], writes, "far", sem, n))
+
+    def sc(x):
+        return ap(x) if isinstance(x, tuple) else x
+
+    def act(out, in_, f, bias=None, scale=None, accum=None):
+        kw = {}
+        if bias is not None: kw["bias"] = sc(bias)
+        if scale is not None: kw["scale"] = sc(scale)
+        if accum is not None: kw["accum_out"] = ap(accum)
+        op("S", lambda: S.activation(ap(out), ap(in_), f, **kw), [in_] + [x for x in (bias, scale) if isinstance(x, tuple)], [out] + ([accum] if accum else []))
+
+    def copy(out, in_, q="V"):
+        if q == "V":
+            op("V", lambda: V.tensor_copy(ap(out), ap(in_)), [in_], [out])
+        else:
+            act(out, in_, AF.Copy)
+
+    def ts(out, in_, s1, op0, s2=None, op1=None):
+        rd = [in_] + [x for x in (s1, s2) if isinstance(x, tuple)]
+        if op1 is None:
+            op("V", lambda: V.tensor_scalar(ap(out), ap(in_), sc(s1), None, op0), rd, [out])
+        else:
+            op("V", lambda: V.tensor_scalar(ap(out), ap(in_), sc(s1), sc(s2), op0, op1), rd, [out])
+
+    def tt(out, a, b, o):
+        op("V", lambda: V.tensor_tensor(ap(out), ap(a), ap(b), o), [a, b], [out])
+
+    def tt_by(out, win, off, b, o):
+        op("V", lambda: V.tensor_tensor(ap(out), ap(win).indirect(ap(off)), ap(b), o), [win, off, b], [out])
+
+    def scan(out, a, b):
+        op("V", lambda: V.tensor_tensor_scan(ap(out), ap(a), ap(b), 0.0, OP.add, OP.add), [a, b], [out])
+
+    def turn(out, in_):
+        op("V", lambda: V.transpose(ap(out), ap(in_)), [in_], [out])
+
+    def fill(out, x):
+        op("V", lambda: V.memset(ap(out), x), [], [out])
+
+    def least(o, i):
+        op("V", lambda: V.tensor_reduce(ap(o), ap(i), AxisListType.X, OP.min, apply_absolute_value=True), [i], [o])
+
+    def iota(out, pattern, base, mult=0):
+        if SCRATCH[out[0]][2] == "int32":
+            op("G", lambda: g.iota(ap(out), pattern, base, mult), [], [out])
+        else:
+            op("G", lambda: g.iota(ap(out), pattern, base, mult, allow_small_or_imprecise_dtypes=True), [], [out])
+
+    def gather(out, win, off, q="V"):
+        if q == "V":
+            op("V", lambda: V.tensor_copy(ap(out), ap(win).indirect(ap(off))), [win, off], [out])
+        else:
+            op("S", lambda: S.activation(ap(out), ap(win).indirect(ap(off)), AF.Copy), [win, off], [out])
+
+    def scatter(win, off, in_):
+        op("V", lambda: V.tensor_copy(ap(win).indirect(ap(off)), ap(in_)), [in_, off], [win])
+
+    def pick(dst, c0, c1, src, w1, off):
+        a, b = reg(dst, c0, c1), reg(src, 0, w1)
+        op("V", lambda: V.tensor_copy(ap(a).bitcast(dt.uint32), ap(b).bitcast(dt.uint32).indirect(ap(off))), [b, off], [a])
+        gather(reg(dst + "s", c0, c1), reg(src + "s", 0, w1), off, "S")
+
+    def both(q, c0, c1):
+        return [reg(q, c0, c1), reg(q + "s", c0, c1)]
+
+    def quant(q, c0, c1, t, e0=0):
+        e1 = e0 + 4 * (c1 - c0)
+        op("V", lambda: V.quantize_mx(T[q][:, c0:c1], T[q + "s"][:, c0:c1], T[t][:, e0:e1]), [reg(t, e0, e1)], both(q, c0, c1))
+
+    def mm(bank, a, a0, b, b0, n, start=True, stop=True):
+        o = reg("ps", 512 * bank, 512 * bank + n)
+        op("P", lambda: PE.matmul_mx(ap(o), T[a][:, a0:a0 + 128], T[a + "s"][:, a0:a0 + 128], T[b][:, b0:b0 + n], T[b + "s"][:, b0:b0 + n], start, stop), both(a, a0, a0 + 128) + both(b, b0, b0 + n), [o], not start)
+
+    def ps(bank, c0, c1, p0=0, p1=128):
+        return reg("ps", 512 * bank + c0, 512 * bank + c1, p0, p1)
+
+    def lanes(src):
+        others = [c for c in T.cores if c != src]
+        off = [c for c in others if topo.chip(c) != topo.chip(src)]
+        on = [c for c in others if topo.chip(c) == topo.chip(src)]
+        out = topo.engines(src, off[0])
+        inn = [e for e in topo.engines(src, on[0]) if e not in out]
+        m = {}
+        for i, c in enumerate(off): m[c] = out[i * (len(out) // len(off)):(i + 1) * (len(out) // len(off))]
+        for i, c in enumerate(on): m[c] = inn[i * (len(inn) // len(on)):(i + 1) * (len(inn) // len(on))]
+        return m
+
+    mine = lanes(core)
+    sources = [T.cores[(rank + 1 + i) % 4] for i in range(3)]
+
+    def slot(dst):
+        return (rank - T.rank_of(dst) - 1) % 4
+
+    def send(sem, pair, reads):
+        def emit():
+            order("G", reads, [])
+            tr = []
+            for c in mine:
+                rid, pid, _ = topo.addr(c)
+                s, d = pair(c)
+                tr.append(RemoteDMATransfer(dst_ids=[DstId(rid=rid, pnc=pid)], dma_engine_mask=sum(1 << e for e in mine[c]), remote_sem=T.sem[sem], src=s, dst=d))
+                count["loc"] += len(mine[c])
+            g.remote_dma_fused(tr, local_sem=T.sem.loc)
+        calls.append(emit)
+
+    incoming = sum(len(lanes(c)[core]) for c in sources)
+
+    def cb(name, c0, c1):
+        return T[name][:, c0:c1].bitcast(dt.uint8)
+
+    def ship(sem, q, s0, n, dst, c0, c1):
+        send(sem, lambda c: (cb(q, s0(c), s0(c) + n), cb("W", dst(c), dst(c) + n)), [reg(q, c0, c1)])
+        send(sem, lambda c: (T[q + "s"][:, s0(c):s0(c) + n], T.Ws[:, dst(c):dst(c) + n]), [reg(q + "s", c0, c1)])
+
+    def as_list(sem, l, c, row, r0):
+        dma("Y", sem, T[l][:, c:c + 16], T[row][0:128:16, r0:r0 + 256], [reg(row, r0, r0 + 256)], [reg(l, c, c + 16)])
+
+    def ti(i):
+        return reg("ti", i, i + 1)
+
+    def tf(i):
+        return reg("tf", i, i + 1)
+
+    for h in range(2):
+        for a in range(4):
+            p0, b0 = 32 * a + 16 * h, 24 * (a // 2)
+            dma("YS"[h], "d_nb", T.nbP[p0:p0 + 16, :], T.nb[:, b0:b0 + 24], [], [reg("nbP", 0, 24, p0, p0 + 16)])
+    for h in range(2):
+        dma("Y", ("d_x", "d_y")[h], T.xt[:, 512 * h:512 * h + 512], T.x[:, 512 * h:512 * h + 512], [], [reg("xt", 512 * h, 512 * h + 512)])
+    dma("S", "d_uv", T.uvs[:, 0:4], T.u[:, 0:4], [], [reg("uvs", 0, 4)])
+    dma("S", "d_uv", T.uvs[:, 16:20], T.v[:, 0:4], [], [reg("uvs", 16, 20)])
+    for h in range(2):
+        for a in range(4):
+            p0 = 32 * a + 16 * h
+            dma("Y", "d_nc", T.nbI[p0:p0 + 16, :], T.nb[:, 12 * a:12 * a + 12], [], [reg("nbI", 0, 12, p0, p0 + 16)])
+    dma("Y", "d_bb", T.bt[:], T.bb[:], [], [reg("bt", 0, 1024)])
+    dma("Y", "d_a", T.at[:], T.a[:], [], [reg("at", 0, 2048)])
+    dma("Y", "d_w", T.wt[:], T.w[:], [], [reg("wt", 0, 512)])
+    pI = reg("pI", 0, 1)
+    iota(reg("pI", 0, 8), [[0, 8]], 0, 1)
+    iota(reg("ID", 0, 256), [[1, 256]], 0)
+    iota(reg("C12", 0, 12), [[1, 3], [48, 4]], 0)
+    for q in range(3):
+        iota(reg("EM", 256 * q, 256 * q + 256), [[0, 256]], 0)
+    act(reg("M", 256 * rank, 256 * rank + 256), reg("ID", 0, 256), AF.Copy)
+    for k, q in ((1, "V"), (2, "S"), (3, "V"), (4, "S")):
+        n = min(256, WC - 256 * k)
+        if q == "V":
+            ts(reg("ID", 256 * k, 256 * k + n), reg("ID", 0, n), 256.0 * k, OP.add)
+        else:
+            act(reg("ID", 256 * k, 256 * k + n), reg("ID", 0, n), AF.Identity, bias=256.0 * k)
+    ts(ti(0), pI, 96, OP.bitwise_and)
+    ts(ti(1), pI, 31, OP.bitwise_and)
+    ts(ti(2), pI, 15, OP.bitwise_and)
+    ts(reg("ti", 8, 16), reg("pI", 0, 8), 3, OP.bitwise_and)
+    ts(tf(4), ti(0), 7.0, OP.mult)
+    copy(tf(3), ti(2))
+    ts(tf(2), ti(0), 2048.0, OP.mult, -MID, OP.add)
+    tt(tf(0), tf(4), pI, OP.add)
+    copy(tf(5), ti(1))
+    ts(tf(8), ti(0), 2.0, OP.mult)
+    tt(tf(9), tf(8), ti(1), OP.add)
+    ts(tf(6), ti(1), 32.0, OP.add)
+    ts(tf(7), ti(2), 3.0, OP.mult)
+    copy(reg("UL", 0, 8), reg("ti", 8, 16))
+    fill(reg("ZB", 0, 256), 0.0)
+    fill(reg("CK", 0, 32), STEP)
+    fill(reg("C1", 0, 32), 1.0)
+    fill(reg("H", 4 * K, 512), 0.0)
+    fill(reg("E1", OWN[0] + 128, FAR), 0.0)
+    for a in range(4):
+        fill(reg("PADD", 0, 1, 32 * a, 32 * a + 32), float(FAR + LC * ((a - rank - 1) % 4 % 3) - 1))
+    act(reg("GCOL", 0, 8), reg("ID", 0, 8), AF.Identity, scale=32.0, bias=tf(0))
+    act(reg("IC", 0, 16), reg("ID", 0, 16), AF.Identity, scale=16.0, bias=tf(3))
+    act(reg("ICS", 0, 8), reg("IC", 0, 8), AF.Identity, scale=-1.0, bias=-0.5)
+    copy(reg("nbp", 0, 24), reg("nbP", 0, 24))
+    gather(reg("FRA", 0, 192), reg("ID", 0, 1024), reg("nbp", 0, 12))
+    gather(reg("FRB", 0, 192), reg("ID", 0, 1024), reg("nbp", 12, 24), "S")
+    copy(reg("FA", 0, 64), reg("FRA", 2, 192, st=3))
+    copy(reg("FA", 64, 128), reg("FRB", 2, 192, st=3))
+    copy(reg("FA", 128, 256, 0, 64), reg("FA", 0, 128, 64, 128))
+    copy(reg("FA", 128, 256, 64, 128), reg("FA", 0, 128, 0, 64))
+    for k in range(2):
+        o = 512 * k
+        gather(reg("uvt", o, o + 128), reg("uvs", 16 * k, 16 * k + 4), reg("UL", 0, 8), "S")
+        copy(reg("uvt", o + 128, o + 256), reg("uvt", o, o + 128), "S")
+        copy(reg("uvt", o + 256, o + 512), reg("uvt", o, o + 256), "S")
+    for h in range(2):
+        quant("Q0", 128 * h, 128 * h + 128, "xt", 512 * h)
+    quant("UV2", 0, 128, "uvt")
+    quant("UV2", 128, 256, "uvt", 512)
+    for c in range(2):
+        mm(c, "Q0", 128 * c, "UV2", 0, 128)
+    for c in range(2):
+        copy(reg("ec", c, c + 1), ps(c, 0, 1), "S")
+    send("r_e", lambda c: (T.ec[:, 0:2], T.eld[slot(c)]), [reg("ec", 0, 2)])
+    arrive("r_e", incoming, reg("eld", 0, 3))
+    dma("Y", "d_q", cb("W", 0, 256), cb("Q0", 0, 256), [reg("Q0", 0, 256)], [reg("W", 0, 256)])
+    dma("Y", "d_q", T.Ws[:, 0:256], T.Q0s[:, 0:256], [reg("Q0s", 0, 256)], [reg("Ws", 0, 256)])
+    dma("Y", "d_p", cb("PK0", 3 * K, PW), cb("Q0", 0, PW - 3 * K), [reg("Q0", 0, PW - 3 * K)], [reg("PK0", 3 * K, PW)])
+    dma("Y", "d_p", T["PK0s"][:, 3 * K:PW], T.Q0s[:, 0:PW - 3 * K], [reg("Q0s", 0, PW - 3 * K)], [reg("PK0s", 3 * K, PW)])
+    for c in range(8):
+        eq = reg("EQ", 256 * c, 256 * c + 256)
+        ts(eq, reg("FA", 0, 256), reg("GCOL", c, c + 1), OP.is_equal)
+        if c < 8 - SCN_S:
+            scan(reg("SC", 128 * c, 128 * c + 128), reg("EQ", 256 * c, 256 * c + 128), reg("EQ", 256 * c + 128, 256 * c + 256))
+            n = reg("SC", 128 * c + 127, 128 * c + 128)
+        else:
+            n = reg("SS", c, c + 1)
+            act(reg("SJ", 0, 256), eq, AF.Copy, accum=n)
+        act(reg("PB", 32 * c, 32 * c + 32), reg("ZB", 0, 32), AF.Sign, bias=n)
+    turn(reg("PR", 0, 256), reg("PB", 0, 256))
+    scan(reg("SCN", 0, 256), reg("PR", 0, 256), reg("ZB", 0, 256))
+    nv = 6 - LEN_S
+    for c in range(nv):
+        ts(reg("LE", 256 * c, 256 * c + 256), reg("SCN", 0, 256), reg("IC", c, c + 1), OP.is_le)
+        scan(reg("LC2", 128 * c, 128 * c + 128), reg("LE", 256 * c, 256 * c + 128), reg("LE", 256 * c + 128, 256 * c + 256))
+    for c in range(nv, 6):
+        act(reg("LJ", 256 * (c % 3), 256 * (c % 3) + 255), reg("SCN", 0, 255), AF.Sign, bias=reg("ICS", c, c + 1), accum=reg("LS", c, c + 1))
+    ts(reg("LST", 0, nv), reg("LC2", 127, 128 * nv, st=128), 255.0, OP.min)
+    ts(reg("LST", nv, 6), reg("LS", nv, 6), -0.5, OP.mult, 127.5, OP.add)
+    send("r_l", lambda c: (T.LST[:, 0:6], T.LA[:, 6 * slot(c):6 * slot(c) + 6]), [reg("LST", 0, 6)])
+    arrive("r_l", incoming, reg("LA", 0, 18))
+    for d in range(4):
+        dma("Y", "d_e", T.EM[32 * d:32 * d + 1, 0:768], T.eld[0:3], [reg("eld", 0, 3)], [reg("EM", 0, 768, 32 * d, 32 * d + 1)])
+    act(reg("SLf", 0, 256), reg("SCN", 0, 256), AF.Identity, bias=reg("PADD", 0, 1))
+    for q in range(4):
+        if q != rank:
+            for d in range(4):
+                dma("Y", "d_m", T.M[32 * d:32 * d + 32, 256 * q:256 * q + 256], T.SLf[32 * q:32 * q + 32, :], [reg("SLf", 0, 256, 32 * q, 32 * q + 32)], [reg("M", 256 * q, 256 * q + 256, 32 * d, 32 * d + 32)])
+    copy(reg("nbo", 0, 12), reg("nbI", 0, 12))
+    for h in range(2):
+        ts(reg("KDL", h, 24, st=2), reg("C12", 0, 12), tf(7), OP.add)
+    gather(reg("FR", 0, 192), reg("ID", 0, 1024), reg("nbo", 0, 12), "S")
+    gather(reg("PDn", 0, 256), reg("FR", 0, 192), reg("KDL", 0, 16), "S")
+    gather(reg("PDn", 256, 384), reg("FR", 0, 192), reg("KDL", 16, 24), "S")
+    turn(reg("PTn", 0, 256), reg("PDn", 0, 256))
+    turn(reg("PTn", 256, 384), reg("PDn", 256, 384))
+    ts(reg("nbK", 0, 8), reg("PTn", 0, 256, st=32), float(-256 * rank), OP.add)
+    copy(reg("nbD", 16, 24), reg("PTn", 256, 384, st=16))
+    copy(reg("nbK", 8, 12), reg("PTn", 256, 384, st=32))
+    m0, m1, n0, n1, n2, n3, n4 = [reg("Ne", 4 * i, 4 * i + 4) for i in range(7)]
+    ts(m0, reg("PTn", 256, 384, st=32), float(1024 - 256 * (rank + 1)), OP.add)
+    ts(m1, m0, 1023, OP.bitwise_and)
+    ts(n0, m0, 127, OP.bitwise_and)
+    ts(n1, m0, 7, OP.logical_shift_right, 1, OP.bitwise_and)
+    tt(n2, n0, m1, OP.add)
+    ts(n3, n1, -127.0, OP.mult)
+    tt(n4, n2, n3, OP.add)
+    copy(reg("nbe", 0, 4), n4)
+    quant("Qb", 0, 256, "bt")
+    mm(5, "UV2", 0, "Q0", 0, 256)
+    mm(4, "UV2", 128, "Qb", 0, 256)
+    for b in range(2):
+        ts(reg("Ft", 64 * b, 64 * b + 64), reg("ID", 0, 64), tf(5 + b), OP.is_lt, 2.0 ** -24, OP.mult)
+    copy(reg("E1", 0, 256), ps(5, 0, 256), "S")
+    for a in range(4):
+        copy(reg("fb", 0, 64, 32 * a, 32 * a + 32), ps(4, 64 * a, 64 * a + 64, 32 * a, 32 * a + 32), "S")
+    act(reg("Fm", 0, 128), reg("Ft", 0, 128), AF.Identity, bias=PRED)
+    copy(reg("Mo", 0, 256), reg("ID", 0, 256), "S")
+    for k in range(2):
+        for i in range(2):
+            ts(reg("FN", 256 * k + 64 * i, 256 * k + 64 * i + 64), reg(("FRA", "FRB")[i], k, 192, st=3), float(-256 * rank), OP.add)
+        copy(reg("FN", 256 * k + 128, 256 * k + 256, 0, 64), reg("FN", 256 * k, 256 * k + 128, 64, 128))
+    for h in range(2):
+        for k in range(3):
+            f, o = ("FN", 256 * k) if k < 2 else ("FA", 0)
+            dma("Y", "d_g", T.nbG[64 * h:64 * h + 64, 16 * k:16 * k + 16], T[f][0:64:16, o:o + 256], [reg(f, o, o + 256, 0, 64)], [reg("nbG", 16 * k, 16 * k + 16, 64 * h, 64 * h + 64)])
+    for h in range(2):
+        copy(reg("DL", h, 32, st=2), reg("IC", 0, 16))
+    iota(reg("VP", 0, 96), [[0, 2], [1, 48]], OWN[2])
+    iota(reg("OFF", 0, 96), [[-16, 3], [0, 2], [-1, 16]], 0)
+    for k in range(2):
+        ts(reg("PAYJ", k, k + 1), tf(9), 1.0 / STEP1, OP.mult, k * 32.0 / STEP1, OP.add)
+    act(reg("OFF", 96, 192), reg("OFF", 0, 96), AF.Identity, bias=reg("PAYJ", 1, 2))
+    act(reg("OFF", 0, 96), reg("OFF", 0, 96), AF.Identity, bias=reg("PAYJ", 0, 1))
+    act(reg("JB", 0, 64), reg("ID", 0, 64), AF.Identity, scale=1024.0, bias=tf(2))
+    act(reg("TB", 0, 4), reg("IC", 0, 4), AF.Identity, scale=-STEP, bias=MID)
+    for t in range(4):
+        copy(reg("bbT", 256 * t, 256 * t + 256), reg("bt", t, 1024, st=4), "S")
+    for d in range(4):
+        copy(reg("LO", 0, 18, 32 * d, 32 * d + 32), reg("LA", 0, 18, 32 * rank, 32 * rank + 32))
+    pick("SND", 0, 288, "Q0", 256, reg("LO", 0, 18))
+    ship("r_c", "SND", lambda c: LC * sources.index(c), LC, lambda c: FAR + LC * slot(c), 0, 3 * LC)
+    arrive("r_c", 2 * incoming, *both("W", FAR, FAR + 3 * LC))
+
+    z0, z1, z2, EG = reg("z0", 0, 64), reg("z1", 0, 64), reg("z2", 0, 64), reg("EG", 0, 64)
+    M = reg("M", 0, 1024)
+    Mo = reg("Mo", 0, 256)
+    C005 = 13421773.0 * 2.0 ** -28
+
+    def payload01():
+        gather(reg("PC", 0, 128), Mo, reg("nbK", 0, 8), "S")
+        act(reg("zK", 0, 64), reg("PC", 64, 128), AF.Identity, scale=512.0, bias=-MID)
+        tt(reg("PAB", 0, 64), reg("zK", 0, 64), reg("PC", 0, 64), OP.add)
+        turn(reg("PAYT", 0, 64), reg("PAB", 0, 64))
+
+    def payload2():
+        gather(reg("PC", 128, 192), M, reg("nbK", 8, 12), "S")
+        tt(reg("PAB", 64, 128), reg("PC", 128, 192), reg("JB", 0, 64), OP.add)
+        turn(reg("PAYT", 64, 128), reg("PAB", 64, 128))
+
+    quant("Qw", 0, 128, "wt")
+    mm(5, "Qw", 0, "Q0", 0, 256)
+    copy(reg("ys", 0, 256), ps(5, 0, 256), "S")
+    for t in range(R):
+        SL, SR = "SL%d" % t, "SR%d" % t
+        PO, J, nf = reg("PO", 10 * t, 10 * t + 9), reg("J", 4 * t, 4 * t + 3), reg("nf", 3 * t, 3 * t + 3)
+        nk, Jn = (2, reg("Ji", 0, 3)) if t == 0 else (1, reg("Dj", 0, 3))
+        wend, w0 = WEND[t], OWN[t]
+        if t == 0:
+            gather(EG, reg("E1", 0, 256), reg("nbK", 0, 4))
+            tt_by(z0, reg("E1", 0, 256), reg("nbK", 4, 8), EG, OP.add)
+            tt_by(z1, reg("EM", 0, 768), reg("nbe", 0, 4), z0, OP.add)
+            payload01()
+            payload2()
+        else:
+            a0 = ARR[t - 1]
+            mm(6, "UV2", 0, "W", a0, 3 * K)
+            copy(reg("E1", a0, a0 + 3 * K), ps(6, 0, 3 * K))
+            tt_by(z1, reg("E1", FAR, wend), reg("EO", 8, 12), z0, OP.add)
+        tt(z2, z1, reg("fb", 0, 64), OP.subtract)
+        act(reg("zr", 0, 64), z2, AF.Abs, bias=TINY)
+        turn(reg("ZT", 0, 64), reg("zr", 0, 64))
+        zr, zs = "zr", "z2"
+        if t == 0:
+            for b in range(2):
+                ts(reg("zB", 32 * b, 32 * b + 32), reg("C1", 0, 32), reg("ZT", 32 * b, 32 * b + 1), OP.mult)
+            turn(reg("zr0", 0, 64), reg("zB", 0, 64))
+            zr = zs = "zr0"
+        for b in range(2):
+            tt(reg("Zc", 256 * b, 256 * b + 64), reg(zr, 0, 64), reg("Fm", 64 * b, 64 * b + 64), OP.mult)
+        for q, d, s, w, x in (("S", 0, 2, 2, 2), ("S", 2, 0, 2, 2), ("S", 0, 1, 1, 1), ("S", 1, 0, 1, 1), ("S", 2, 3, 1, 1), ("S", 3, 2, 1, 1), ("S", 0, 3, 1, 3), ("V", 3, 0, 1, 3), ("V", 1, 2, 1, 3), ("S", 2, 1, 1, 3)):
+            o = reg("Zc", 64 * x, 64 * x + 64, 32 * d, 32 * d + 32 * w)
+            i = reg(zs if q == "S" else zr, 0, 64, 32 * s, 32 * s + 32 * w)
+            f = PRED if s > d else 1.0
+            if q == "S":
+                if t == 0:
+                    act(o, i, AF.Copy, scale=f)
+                else:
+                    act(o, i, AF.Abs, scale=f, bias=TINY * f)
+            elif s > d:
+                ts(o, i, f, OP.mult)
+            else:
+                copy(o, i)
+        ts(reg("ZN", 0, 1), reg("ZT", 32, 33), -UP, OP.mult)
+        ts(reg("MK", 256, 256 + VPART), reg("Zc", 64, 64 + VPART), reg("ZT", 32, 33), OP.is_ge, 1.0, OP.subtract)
+        act(reg("MK", 256 + VPART, 512), reg("Zc", 64 + VPART, 320), AF.Sign, scale=UP, bias=reg("ZN", 0, 1))
+        for h in range(2):
+            ts(reg("MK", 128 * h, 128 * h + 128), reg("Zc", 128 * h, 128 * h + 128), reg("ZT", 0, 1), OP.is_ge)
+        act(reg("SJ", 0, 256), reg("MK", 256, 512), AF.Sign, bias=1.0, accum=reg("SS", 0, 1))
+        scan(reg("RS", 0, 128), reg("MK", 0, 128), reg("MK", 128, 256))
+        if t == 0:
+            for k in range(2):
+                o = 64 * k
+                ts(reg("KB", o, o + 32), reg("CK", 0, 32), reg("RS", 127, 128), OP.mult, reg("PAYT", o, o + 1), OP.add)
+                act(reg("KB", o + 32, o + 64), reg("CK", 0, 32), AF.Identity, scale=reg("SS", 0, 1), bias=reg("PAYT", o + 32, o + 33))
+            turn(reg("KEY", 0, 128), reg("KB", 0, 128))
+            for c in range(3):
+                o, tb = reg("DK", 128 * c, 128 * c + 128), reg("TB", c, c + 1)
+                if c == 2:
+                    ts(o, reg("KEY", 0, 128), tb, OP.add)
+                else:
+                    act(o, reg("KEY", 0, 128), AF.Identity, bias=tb)
+            for c in range(3):
+                for k in range(2):
+                    least(reg("R0", 3 * k + c, 3 * k + c + 1), reg("DK", 128 * c + 64 * k, 128 * c + 64 * k + 64))
+        else:
+            for c in range(3):
+                o = 64 * c
+                ts(reg("KB", o, o + 32), reg("OFF", 32 * c, 32 * c + 32), reg("RS", 127, 128), OP.add)
+                act(reg("KB", o + 32, o + 64), reg("OFF", 96 + 32 * c, 128 + 32 * c), AF.Identity, bias=reg("SS", 0, 1))
+            for c in range(3):
+                o = 64 * c
+                turn(reg("KEY", o, o + 64), reg("KB", o, o + 64))
+                least(reg("R0", c, c + 1), reg("KEY", o, o + 64))
+        n3 = 3 * nk
+        for d in range(2):
+            tt(reg("R1", 0, n3, 64 * d, 64 * d + 64), reg("R0", 0, n3, 64 * d, 64 * d + 64), reg("R0", 0, n3, 64 - 64 * d, 128 - 64 * d), OP.min)
+        Rd = "Ri" if t == 0 else "Rf"
+        for d in range(4):
+            s = d ^ 1
+            tt(reg(Rd, 0, n3, 32 * d, 32 * d + 32), reg("R1", 0, n3, 32 * d, 32 * d + 32), reg("R1", 0, n3, 32 * s, 32 * s + 32), OP.min)
+        if t == 0:
+            ts(reg("Di", 0, 3), reg("Ri", 0, 3), 511, OP.bitwise_and)
+            ts(reg("Di", 3, 6), reg("Ri", 0, 3), 9, OP.logical_shift_right)
+            ts(reg("Di", 6, 9), reg("Ri", 3, 6), 1023, OP.bitwise_and)
+            copy(PO, reg("Di", 0, 9))
+            pick("PK0", 0, 144, "W", wend, PO)
+            ts(Jn, reg("Ri", 3, 6), 10, OP.logical_shift_right)
+            copy(J, Jn)
+        else:
+            ts(J, reg("Rf", 0, 3), STEP1, OP.mult)
+            ts(Jn, reg("Rf", 0, 3), STEP1, OP.mult)
+        if t < 2:
+            ts(reg(SL, 0, 3), Jn, float(256 * rank), OP.add)
+            send("r_s%d" % t, lambda c, SL=SL, SR=SR: (T[SL][:, 0:3], T[SR][:, 3 * slot(c):3 * slot(c) + 3]), [reg(SL, 0, 3)])
+            arrive("r_s%d" % t, incoming, reg(SR, 0, 9))
+        if t < 2:
+            scatter(Mo, J, reg("ID", w0, w0 + K))
+        else:
+            ts(reg("Dj", 8, 11), Jn, 240, OP.bitwise_and)
+            tt(reg("Dj", 4, 7), Jn, reg("Dj", 8, 11), OP.add)
+            copy(reg("JD", 0, 3), reg("Dj", 4, 7))
+            ts(reg("JD", 3, 6), reg("Dj", 4, 7), 16.0, OP.add)
+            scatter(reg("MoD", 0, 512), reg("JD", 0, 6), reg("VP", 0, 96))
+            for h in range(4):
+                turn(reg("FT", 128 * h, 128 * h + 128), reg("MoD", 128 * h, 128 * h + 128))
+            for h in range(2):
+                copy(reg("FO", 8 * h, 8 * h + 8), reg("FT", 256 * h, 256 * h + 256, st=32))
+        if t == 0:
+            quant("Qa", 0, 256, "at")
+            quant("Qa", 256, 512, "at", 1024)
+            for b in range(4 - INP):
+                mm(b, "Qa", 128 * b, "PK0", 0, 3 * K)
+            for b in range(4 - INP, 4):
+                for k in range(3):
+                    mm(b, "Qa", 128 * b, "PK0", K * k, 128, k == 0, k == 2)
+            for b in range(4):
+                s0, s1, s2, s3 = [reg("SU", 192 * k + K * b, 192 * k + K * b + K) for k in range(4)]
+                if b < 4 - INP:
+                    copy(s0, ps(b, 0, K), "S")
+                    tt(s1, ps(b, K, 2 * K), s0, OP.add)
+                    tt(s2, ps(b, 2 * K, 3 * K), s1, OP.add)
+                else:
+                    s2 = ps(b, 0, K)
+                act(s3, s2, AF.Copy, scale=C005)
+                tt_by(reg("H", b, 4 * K, st=4), reg("bbT", 256 * b, 256 * b + 256), J, s3, OP.add)
+        else:
+            for b in range(4):
+                gather(reg("G4", K * b, K * b + K), reg("bbT", 256 * b, 256 * b + 256), J, "S")
+            for b in range(4):
+                tt_by(reg("H", b, 4 * K, st=4), reg("ST", 256 * b, 256 * b + 256), J, reg("G4", K * b, K * b + K), OP.add)
+        if t == 0:
+            mm(7, "UV2", 0, "W", FAR, 3 * LC)
+            copy(reg("E1", FAR, FAR + 3 * LC), ps(7, 0, 3 * LC), "S")
+        quant("W", w0, w0 + 128, "H")
+        if t < 2:
+            ship("r_n%d" % t, "W", lambda c, w0=w0: w0, K, lambda c, t=t: ARR[t] + K * slot(c), w0, w0 + K)
+            arrive("r_n%d" % t, 2 * incoming, *both("W", ARR[t], ARR[t] + 3 * K))
+            u = t + 1
+            PA = "PA%d" % u
+            mm(7, "UV2", 0, "W", w0, 128)
+            copy(reg("en", K * t, K * t + K), ps(7, 0, K), "S")
+            scatter(reg("E1", 0, 256), J, reg("en", K * t, K * t + K))
+            gather(EG, reg("E1", 0, 256), reg("nbK", 0, 4))
+            tt_by(z0, reg("E1", 0, 256), reg("nbK", 4, 8), EG, OP.add)
+            w = 256 // NP
+            for k in range(2):
+                gather(reg("LRo", 256 * k, 256 * k + 256), Mo, reg("nbG", 16 * k, 16 * k + 16), "S")
+                as_list("d_l%d" % (3 * t + k), "LIo", 32 * t + 16 * k, "LRo", 256 * k)
+                o = 48 * t + 16 * k
+                copy(reg("Lu", o, o + 16), reg("LIo", 32 * t + 16 * k, 32 * t + 16 * k + 16))
+                for h in range(NP):
+                    pick(PA, 256 * k + w * h, 256 * k + w * h + w, "W", w0 + K, reg("Lu", o + w // 16 * h, o + w // 16 * (h + 1)))
+                for b in range(4):
+                    mm(b, "Qa", 128 * b, PA, 256 * k, 256, k == 0, False)
+            scatter(M, reg(SR, 0, 9), reg("ID", ARR[t], ARR[t] + 3 * K))
+            gather(reg("PD", 256, 384), M, reg("nbD", 16, 24), "S")
+            turn(reg("PT", 256, 384), reg("PD", 256, 384))
+            ts(reg("EO", 8, 12), reg("PT", 256, 384, st=32), float(-FAR), OP.add)
+            gather(reg("LRf", 0, 256), M, reg("nbG", 32, 48), "S")
+            as_list("d_l%d" % (3 * t + 2), "LIf", 16 * t, "LRf", 0)
+            o = 48 * t + 32
+            copy(reg("Lu", o, o + 16), reg("LIf", 16 * t, 16 * t + 16))
+            for h in range(NP):
+                pick(PA, 512 + w * h, 512 + w * h + w, "W", WEND[u], reg("Lu", o + w // 16 * h, o + w // 16 * (h + 1)))
+            for b in range(4):
+                mm(b, "Qa", 128 * b, PA, 512, 256, False, True)
+            for b in range(4):
+                act(reg("ST", 256 * b, 256 * b + 256), ps(b, 0, 256), AF.Copy, scale=C005)
+        else:
+            for h in range(2):
+                pick("FIN", 128 * h, 128 * h + 128, "W", WC, reg("FO", 8 * h, 8 * h + 8))
+        copy(nf, Jn)
+        for c in range(3):
+            dma("Y", "d_nd", T.nd[t:t + 1, 16 * c:16 * c + 16], T.nf[0:16, 3 * t + c:3 * t + c + 1], [nf], [])
+        if t == 1:
+            for h in range(4):
+                gather(reg("MoD", 128 * h, 128 * h + 128), Mo, reg("DL", 8 * h, 8 * h + 8), "S")
+        mm(4, "Qw", 0, "W", w0, 128)
+        copy(reg("yn", K * t, K * t + K), ps(4, 0, K), "S")
+        scatter(reg("ys", 0, 256), J, reg("yn", K * t, K * t + K))
+
+    dma("Y", "d_out", T.oc[:, 0:1024], cb("FIN", 0, 256), [reg("FIN", 0, 256)], [])
+    for k in range(4):
+        dma("YYSS"[k], "d_out", T.osc[4 * k:4 * k + 4, 0:256], T.FINs[32 * k:32 * k + 4, 0:256], [reg("FINs", 0, 256)], [])
+    for h in range(2):
+        dma("YS"[h], "d_out", T.y[:, 128 * h:128 * h + 128], T.ys[:, 128 * h:128 * h + 128], [reg("ys", 128 * h, 128 * h + 128)], [])
+    for i in ORDER:
+        calls[i]()
+    for s in ("v", "s", "p", "gq", "d_q", "d_g", "d_nd", "d_out", "loc"):
+        if know["G"].get(s, 0) < count[s]:
+            g.wait_ge(T.sem[s], count[s])

@@ -1,41 +1,35 @@
 from concourse.bass import DstId, RemoteDMATransfer
-from concourse.mybir import AluOpType as OP, AxisListType, ActivationFunctionType as AF, dt
+from concourse.mybir import AluOpType as OP, ActivationFunctionType as AF, dt
 
 P, K, R, LC = 256, 48, 3, 96
 OWN = [P, P + K]
-FAR = P + K + 128
+FAR = 448
 ARR = [FAR + 3 * LC, FAR + 3 * LC + 3 * K]
 OWN.append(ARR[1] + 3 * K)
 WEND = [ARR[0], ARR[1], OWN[2]]
 WC = OWN[2] + 128
-PW = 2 * K + 128
 TINY = 2.0 ** -122
 PRED = 1.0 - 2.0 ** -24
-STEP, MID = 2.0 ** 19, 2.0 ** 24
-STEP1 = 512.0
-UP = 2.0 ** 23
-VPART = 128
-NP = 2
-INP = 2
-SCN_S = 2
+BIG = 2048.0
 LEN_S = 3
+VX = 2
 ORDER = [int(_i) for _i in """
-53 10 8 23 48 11 9 0 6 4 24 1 5 2 37 3 7 34 12 13 47 14 15 38 16 36 17 18 41 39 19 25 189 46 20 21 30 31 26 22 32 67 57 60 27 74 61 62 73 68 188 33 85 69 63 86 64 58 143 83 84 146 65 66 182 75 77 28 78 185 144 59 105 163 195 108 70 87 106 79 90 93 80 81 88 96 91 109 99 102 107 94 89 97 92 100 110 95 103 98 145 101 54 104 55 56 35 111 148 150 112 82 42 129 126 127 113 128 147 115 119 117 114 116 120 154 118 149 121 122 71 123 72 124 157 155 167 162 156 76 151 130 159 158 164 212 173 160 131 132 133 213 134 135 161 136 168 137 45 169 138 170 139 214 171 140 141 29 50 222 165 166 125 223 153 215 216 200 224 201 172 203 202 225 226 142 240 40 227 205 207 204 238 229 230 231 206 232 234 233 235 236 217 228 237 239 241 194 219 242 218 243 198 220 244 221 49 246 174 247 245 248 250 196 249 175 251 177 252 254 208 253 178 303 255 197 256 259 257 258 260 152 261 199 262 263 264 266 304 265 43 267 268 269 176 270 279 272 271 281 179 273 282 280 289 283 284 285 286 180 275 274 183 294 181 52 184 290 44 295 291 276 296 292 278 297 287 51 293 288 298 299 301 300 302 314 355 191 305 306 309 307 209 359 277 336 187 315 210 356 357 358 325 326 310 311 192 337 186 190 312 340 338 316 339 317 341 308 318 319 320 327 193 360 313 362 329 330 331 322 363 328 321 211 323 364 324 342 344 365 343 366 370 333 371 367 372 332 377 373 374 375 334 378 376 369 380 379 368 381 382 383 385 384 345 346 386 388 387 390 389 347 392 391 393 395 397 394 348 396 351 398 349 399 400 352 401 403 404 402 353 405 406 411 412 407 410 335 350 408 469 361 470 471 415 413 414 472 354 416 417 428 418 419 439 429 420 423 477 421 473 440 409 424 450 478 474 430 451 425 431 433 432 434 426 441 422 452 454 480 427 435 443 475 453 481 442 482 479 483 455 444 437 436 445 476 438 484 488 489 446 485 490 496 495 487 491 448 447 493 494 492 498 497 486 500 499 456 501 503 502 457 458 460 504 506 459 508 505 461 510 507 509 511 513 515 462 512 514 465 516 463 449 517 518 466 519 520 464 521 522 524 523 467 525 549 526 550 551 537 536 552 541 527 528 539 538 468 540 529 542 543 530 531 544 553 533 532 534 546 554 535 545 547 548 555 556 559 557 560 558 561 562
+14 12 19 46 6 3 11 2 21 13 10 7 5 48 8 1 33 9 4 0 15 18 20 31 16 58 53 32 78 47 51 34 30 24 39 59 143 36 50 35 27 54 60 40 149 41 56 29 42 23 26 25 150 28 57 151 67 75 43 68 61 69 44 37 62 63 71 52 79 55 70 64 128 72 66 180 49 45 65 159 73 76 99 179 91 74 158 38 157 160 95 17 87 80 103 77 92 100 88 130 104 131 101 96 102 141 126 133 127 83 106 152 93 89 84 97 134 98 140 105 94 90 85 86 129 144 142 107 161 181 108 135 132 111 115 109 113 112 116 173 182 137 114 176 138 110 139 117 136 174 177 147 146 118 148 145 119 175 178 120 122 153 186 22 187 125 171 124 82 123 81 188 189 172 162 121 190 183 191 200 192 202 193 164 194 195 163 165 198 201 199 203 197 166 196 167 206 184 204 168 207 169 205 210 154 208 211 209 155 214 156 212 213 185 215 216 217 219 218 225 220 221 227 238 223 224 241 239 245 170 228 244 226 249 278 230 246 231 229 250 233 277 232 253 279 240 235 248 234 252 236 222 237 247 293 242 251 243 310 254 257 256 258 255 264 266 259 262 265 260 294 263 261 267 268 280 297 295 281 269 272 313 270 298 273 282 274 314 296 283 275 315 288 287 284 276 285 271 316 290 317 291 299 318 286 301 319 300 292 320 328 329 324 332 325 326 321 304 330 322 323 327 331 333 334 303 335 308 289 337 336 307 302 338 339 341 340 305 342 345 306 343 344 309 346 347 348 349 350 353 354 356 351 355 358 357 360 371 359 361 372 362 352 387 363 407 366 373 364 408 367 388 368 409 389 369 391 390 374 370 365 375 376 410 392 405 312 382 406 411 379 412 413 378 381 377 414 417 420 380 423 421 424 415 425 422 416 418 386 419 426 393 427 428 384 394 395 385 429 431 399 430 432 433 398 435 434 403 436 437 397 438 439 440 402 383 441 401 443 460 396 462 461 442 444 404 311 449 450 447 448 453 400 454 445 452 451 446 455 458 463 457 456 464 459 466 465 468 467 471 470 469
 """.split()]
 
 BUF = {
-    "float32": "ID:%d JB:64 Fm:128 Ft:128 FRA:192 FRB:192 FR:192 SLf:256 LJ:768 SJ:256 Mo:256 MoD:512 LRo:512 LRf:256 LIo:64 LIf:32 en:96 G4:192 ST:1024 M:1024 ec:2 EM:768 E1:%d fb:64 PC:192 PAB:128 PAYT:128 PDn:384 PTn:384 PD:384 PT:384 EG:64 zK:64 z0:64 z1:64 z2:64 zr:64 ZT:64 zB:64 zr0:64 Zc:320 KB:192 KEY:192 DK:384 RS:128 nf:9 SU:768 FT:512 ys:256 yn:144" % (WC, OWN[2]),
-    "bfloat16": "ZB:256 xt:1024 bt:1024 at:2048 wt:512 uvs:32 uvt:1024 bbT:1024 EQ:2048 SC:1024 PB:256 PR:256 SCN:256 LE:1536 LC2:768 MK:512 H:512",
-    "int32": "pI:8 ti:24 nbI:12 nbP:24 Ne:28 Ri:6 Di:9 Ji:3 Dj:12",
-    "uint16": "UL:8 DL:32 FN:512 nbG:48 Lu:96 JD:8 KDL:24 nbp:24 nbo:12 nbe:4 nbD:24 nbK:12 FA:256 LST:6 LA:18 LO:18 EO:12 PO:30 J:12 SL0:4 SL1:4 SR0:9 SR1:9 FO:16",
+    "float32": "ID:%d Fm:64 Ft:32 FR:384 SLf:256 LJ:768 Mo:256 LRo:512 LRf:256 LIo:64 LIf:32 en:96 G4:192 ST:1024 M:1024 ec:2 TAB:1024 E1:%d fb:64 PC:64 PAB:64 PAYT:128 LQ:256 TG:64 PD:128 PT:128 EG:64 zK:64 z0:64 z1:64 z2:64 ZT:64 zB:64 Zc:320 OF:384 TF:384 XF:384 RS:256 YJ:9 SU:192 FT:256 ys:256 yn:144" % (WC, OWN[2]),
+    "bfloat16": "xt:1024 bt:1024 at:2048 wt:512 uz:512 bbT:1024 EQ:1536 SC:768 PB:256 PR:256 SCN:256 LE:1536 LC2:768 MK:512 H:512 POS:96 OH:192 TH:192 XH:192 M16:80 LM:256 LA1:64 LA2:66",
+    "int32": "ti:4 nbP:24 Ri:6 Di:9",
+    "uint16": "UL:16 FN:512 nbG:48 Lu:96 nbp:24 nbe:4 nbD:8 nbK:12 FA:256 LST:6 LA:18 EO:4 PO:10 PF:4 J:12 SL0:4 SL1:4 SR0:9 SR1:9 FO:16",
 }
-SMALL = "C12:12 tf:12 GCOL:8 IC:16 ICS:8 TB:4 CK:32 C1:32 PADD:4 LS:8 SS:8 VP:96 PAYJ:4 OFF:192 ZN:4 Rf:4 R0:8 R1:8"
+SMALL = "tf:12 GCOL:8 IC:16 ICS:8 C1:32 PADD:4 LS:8 PAY:4 PJ:4"
 PART = {}
 _n = 0
 for _b in SMALL.split():
     PART[_b.split(":")[0]] = _n
     _n += int(_b.split(":")[1])
-QBUF = "Q0:256 Qb:256 Qa:512 Qw:128 UV2:256 SND:288 W:%d PK0:%d PA1:768 PA2:768 FIN:256" % (WC, PW)
+QBUF = "Q0:256 Qb:256 Qa:512 Qw:128 UV1:128 UV2:256 SND:288 W:%d PK0:256 PA1:768 PA2:768 FIN:256" % WC
 SCRATCH = {"eld": ("dram", [3, 128, 2], "float32"), "ps": ("psum", [128, 4096], "float32"), "KC": ("sbuf", [128, _n], "float32")}
 for _d, _s in BUF.items():
     for _b in _s.split():
@@ -43,7 +37,7 @@ for _d, _s in BUF.items():
 for _b in QBUF.split():
     SCRATCH[_b.split(":")[0]] = ("sbuf", [128, int(_b.split(":")[1])], "float8_e4m3fn_x4")
     SCRATCH[_b.split(":")[0] + "s"] = ("sbuf", [128, int(_b.split(":")[1])], "uint8")
-SEMAPHORES = "v s p gq d_nb d_nc d_x d_y d_p d_uv d_bb d_a d_w d_q d_m d_e d_nd d_out d_g d_l0 d_l1 d_l2 d_l3 d_l4 d_l5 r_e r_l r_c r_s0 r_s1 r_n0 r_n1 loc".split()
+SEMAPHORES = "v s p gq d_nb d_x d_y d_u d_v d_bb d_a d_w d_q d_m d_e d_nd d_out d_g d_h d_l0 d_l1 d_l2 d_l3 r_e r_l r_c r_s0 r_s1 r_n0 r_n1 loc".split()
 
 
 def rank_program(g, core, T, topo):
@@ -56,7 +50,7 @@ def rank_program(g, core, T, topo):
     count = {s: 0 for s in SEMAPHORES}
     total = {s: 0 for s in SEMAPHORES}
     know = {q: {} for q in queue}
-    snaps, touched, calls = {}, {}, []
+    snaps, touched, calls, across = {}, {}, [], [0]
 
     def reg(name, c0, c1, p0=0, p1=128, st=1):
         if name in PART:
@@ -69,12 +63,12 @@ def rank_program(g, core, T, topo):
 
     def meet(a, b):
         if a[0] == "ps":
-            return a[3] // 512 == b[3] // 512
+            return a[3] // 512 <= (b[4] - 1) // 512 and b[3] // 512 <= (a[4] - 1) // 512
         if a[2] <= b[1] or b[2] <= a[1] or a[4] <= b[3] or b[4] <= a[3]:
             return False
         return not (a[5] == b[5] > 1 and a[3] % a[5] != b[3] % b[5])
 
-    def order(q, reads, writes, acc=False):
+    def order(q, reads, writes, acc):
         want = {}
         for r, w in [(r, False) for r in reads] + [(r, True) for r in writes]:
             for (o, ow, oq, sem, val) in touched.get(r[0], []):
@@ -96,39 +90,46 @@ def rank_program(g, core, T, topo):
         for r in writes:
             touched.setdefault(r[0], []).append((r, True, q, sem, val))
 
-    def op(q, fn, reads, writes, acc=False):
-        s = sem_of[q]
-
-        def emit():
-            order(q, reads, writes, acc)
+    def issue(kind, q, s, reads, writes, x, fn):
+        if kind == "far":
+            return note([], writes, "far", s, x)
+        order(q, reads, writes, x is True)
+        if q == "V" and x is False and know[q].get(s, 0) < across[0]:
+            V.wait_ge(T.sem[s], across[0])
+            know[q][s] = across[0]
+        if kind == "send":
+            fn()
+        elif kind == "dma":
+            count[s] += 16
+            fn().then_inc(T.sem[s], 16)
+            note(reads, writes, "dma", s, total[s])
+        else:
             count[s] += 1
             fn().then_inc(T.sem[s], 1)
             snaps[(s, count[s])] = dict(know[q])
             note(reads, writes, q, s, count[s])
-        calls.append(emit)
+            if x == "across":
+                across[0] = count[s]
+
+    def op(q, fn, reads, writes, mark=False):
+        calls.append(("op", q, sem_of[q], reads, writes, mark, fn))
 
     def dma(q, sem, out, in_, reads, writes):
         total[sem] += 16
-
-        def emit():
-            order(q, reads, writes)
-            count[sem] += 16
-            queue[q].dma_start(out, in_).then_inc(T.sem[sem], 16)
-            note(reads, writes, "dma", sem, total[sem])
-        calls.append(emit)
+        calls.append(("dma", q, sem, reads, writes, False, lambda: queue[q].dma_start(out, in_)))
 
     def arrive(sem, n, *writes):
-        calls.append(lambda: note([], writes, "far", sem, n))
+        calls.append(("far", "", sem, [], list(writes), n, None))
 
     def sc(x):
         return ap(x) if isinstance(x, tuple) else x
 
-    def act(out, in_, f, bias=None, scale=None, accum=None):
+    def act(out, in_, f, bias=None, scale=None, accum=None, by=None):
         kw = {}
         if bias is not None: kw["bias"] = sc(bias)
         if scale is not None: kw["scale"] = sc(scale)
         if accum is not None: kw["accum_out"] = ap(accum)
-        op("S", lambda: S.activation(ap(out), ap(in_), f, **kw), [in_] + [x for x in (bias, scale) if isinstance(x, tuple)], [out] + ([accum] if accum else []))
+        op("S", lambda: S.activation(ap(out), ap(in_).indirect(ap(by)) if by else ap(in_), f, **kw), [in_] + [x for x in (bias, scale, by) if isinstance(x, tuple)], [out] + ([accum] if accum else []))
 
     def copy(out, in_, q="V"):
         if q == "V":
@@ -144,22 +145,22 @@ def rank_program(g, core, T, topo):
             op("V", lambda: V.tensor_scalar(ap(out), ap(in_), sc(s1), sc(s2), op0, op1), rd, [out])
 
     def tt(out, a, b, o):
-        op("V", lambda: V.tensor_tensor(ap(out), ap(a), ap(b), o), [a, b], [out])
+        op("V", lambda: V.tensor_tensor(ap(out), ap(a), ap(b), o), [a, b], [out], a[1] != b[1] and "across")
 
     def tt_by(out, win, off, b, o):
         op("V", lambda: V.tensor_tensor(ap(out), ap(win).indirect(ap(off)), ap(b), o), [win, off, b], [out])
 
-    def scan(out, a, b):
-        op("V", lambda: V.tensor_tensor_scan(ap(out), ap(a), ap(b), 0.0, OP.add, OP.add), [a, b], [out])
+    def scan(out, a, b, o=OP.add):
+        op("V", lambda: V.tensor_tensor_scan(ap(out), ap(a), ap(b), 0.0, OP.add, o), [a, b], [out], a[1] != b[1] and "across")
+
+    def latch(out, row, n):
+        scan(out, reg("LM", 0, n), row, OP.min)
 
     def turn(out, in_):
-        op("V", lambda: V.transpose(ap(out), ap(in_)), [in_], [out])
+        op("V", lambda: V.transpose(ap(out), ap(in_)), [in_], [out], "turn")
 
     def fill(out, x):
         op("V", lambda: V.memset(ap(out), x), [], [out])
-
-    def least(o, i):
-        op("V", lambda: V.tensor_reduce(ap(o), ap(i), AxisListType.X, OP.min, apply_absolute_value=True), [i], [o])
 
     def iota(out, pattern, base, mult=0):
         if SCRATCH[out[0]][2] == "int32":
@@ -171,15 +172,15 @@ def rank_program(g, core, T, topo):
         if q == "V":
             op("V", lambda: V.tensor_copy(ap(out), ap(win).indirect(ap(off))), [win, off], [out])
         else:
-            op("S", lambda: S.activation(ap(out), ap(win).indirect(ap(off)), AF.Copy), [win, off], [out])
+            act(out, win, AF.Copy, by=off)
 
     def scatter(win, off, in_):
         op("V", lambda: V.tensor_copy(ap(win).indirect(ap(off)), ap(in_)), [in_, off], [win])
 
-    def pick(dst, c0, c1, src, w1, off):
-        a, b = reg(dst, c0, c1), reg(src, 0, w1)
+    def pick(dst, c0, c1, src, w0, w1, off):
+        a, b = reg(dst, c0, c1), reg(src, w0, w1)
         op("V", lambda: V.tensor_copy(ap(a).bitcast(dt.uint32), ap(b).bitcast(dt.uint32).indirect(ap(off))), [b, off], [a])
-        gather(reg(dst + "s", c0, c1), reg(src + "s", 0, w1), off, "S")
+        gather(reg(dst + "s", c0, c1), reg(src + "s", w0, w1), off, "S")
 
     def both(q, c0, c1):
         return [reg(q, c0, c1), reg(q + "s", c0, c1)]
@@ -192,8 +193,8 @@ def rank_program(g, core, T, topo):
         o = reg("ps", 512 * bank, 512 * bank + n)
         op("P", lambda: PE.matmul_mx(ap(o), T[a][:, a0:a0 + 128], T[a + "s"][:, a0:a0 + 128], T[b][:, b0:b0 + n], T[b + "s"][:, b0:b0 + n], start, stop), both(a, a0, a0 + 128) + both(b, b0, b0 + n), [o], not start)
 
-    def ps(bank, c0, c1, p0=0, p1=128):
-        return reg("ps", 512 * bank + c0, 512 * bank + c1, p0, p1)
+    def ps(bank, c0, c1, p0=0, p1=128, st=1):
+        return reg("ps", 512 * bank + c0, 512 * bank + c1, p0, p1, st)
 
     def lanes(src):
         others = [c for c in T.cores if c != src]
@@ -208,13 +209,13 @@ def rank_program(g, core, T, topo):
 
     mine = lanes(core)
     sources = [T.cores[(rank + 1 + i) % 4] for i in range(3)]
+    rest = [q for q in range(4) if q != rank]
 
     def slot(dst):
         return (rank - T.rank_of(dst) - 1) % 4
 
     def send(sem, pair, reads):
         def emit():
-            order("G", reads, [])
             tr = []
             for c in mine:
                 rid, pid, _ = topo.addr(c)
@@ -222,7 +223,7 @@ def rank_program(g, core, T, topo):
                 tr.append(RemoteDMATransfer(dst_ids=[DstId(rid=rid, pnc=pid)], dma_engine_mask=sum(1 << e for e in mine[c]), remote_sem=T.sem[sem], src=s, dst=d))
                 count["loc"] += len(mine[c])
             g.remote_dma_fused(tr, local_sem=T.sem.loc)
-        calls.append(emit)
+        calls.append(("send", "G", sem, reads, [], False, emit))
 
     incoming = sum(len(lanes(c)[core]) for c in sources)
 
@@ -233,105 +234,100 @@ def rank_program(g, core, T, topo):
         send(sem, lambda c: (cb(q, s0(c), s0(c) + n), cb("W", dst(c), dst(c) + n)), [reg(q, c0, c1)])
         send(sem, lambda c: (T[q + "s"][:, s0(c):s0(c) + n], T.Ws[:, dst(c):dst(c) + n]), [reg(q + "s", c0, c1)])
 
-    def as_list(sem, l, c, row, r0):
-        dma("Y", sem, T[l][:, c:c + 16], T[row][0:128:16, r0:r0 + 256], [reg(row, r0, r0 + 256)], [reg(l, c, c + 16)])
-
     def ti(i):
         return reg("ti", i, i + 1)
 
     def tf(i):
         return reg("tf", i, i + 1)
 
-    for h in range(2):
-        for a in range(4):
-            p0, b0 = 32 * a + 16 * h, 24 * (a // 2)
-            dma("YS"[h], "d_nb", T.nbP[p0:p0 + 16, :], T.nb[:, b0:b0 + 24], [], [reg("nbP", 0, 24, p0, p0 + 16)])
-    for h in range(2):
-        dma("Y", ("d_x", "d_y")[h], T.xt[:, 512 * h:512 * h + 512], T.x[:, 512 * h:512 * h + 512], [], [reg("xt", 512 * h, 512 * h + 512)])
-    dma("S", "d_uv", T.uvs[:, 0:4], T.u[:, 0:4], [], [reg("uvs", 0, 4)])
-    dma("S", "d_uv", T.uvs[:, 16:20], T.v[:, 0:4], [], [reg("uvs", 16, 20)])
+    def blk(name, c0, c1, a, n=1, st=1):
+        return reg(name, c0, c1, 32 * a, 32 * (a + n), st)
+
     for h in range(2):
         for a in range(4):
             p0 = 32 * a + 16 * h
-            dma("Y", "d_nc", T.nbI[p0:p0 + 16, :], T.nb[:, 12 * a:12 * a + 12], [], [reg("nbI", 0, 12, p0, p0 + 16)])
+            if a % 2 == 0:
+                dma("YS"[h], "d_nb", T.nbP[p0:p0 + 16, :], T.nb[:, 12 * a:12 * a + 24], [], [reg("nbP", 0, 24, p0, p0 + 16)])
+            else:
+                for k in range(2):
+                    dma("YS"[h], "d_nb", T.nbP[p0:p0 + 16, 12 * k:12 * k + 12], T.nb[:, 12 * (a - k):12 * (a - k) + 12], [], [reg("nbP", 12 * k, 12 * k + 12, p0, p0 + 16)])
+    for h in range(2):
+        dma("Y", ("d_x", "d_y")[h], T.xt[:, 512 * h:512 * h + 512], T.x[:, 512 * h:512 * h + 512], [], [reg("xt", 512 * h, 512 * h + 512)])
+    dma("S", "d_u", T.uz[:, 0:16], T.u[:, 0:16], [], [reg("uz", 0, 16)])
+    dma("S", "d_v", T.uz[:, 16:32], T.v[:, 0:16], [], [reg("uz", 16, 32)])
     dma("Y", "d_bb", T.bt[:], T.bb[:], [], [reg("bt", 0, 1024)])
     dma("Y", "d_a", T.at[:], T.a[:], [], [reg("at", 0, 2048)])
     dma("Y", "d_w", T.wt[:], T.w[:], [], [reg("wt", 0, 512)])
-    pI = reg("pI", 0, 1)
-    iota(reg("pI", 0, 8), [[0, 8]], 0, 1)
+    pI = ti(3)
+    iota(pI, [[0, 1]], 0, 1)
     iota(reg("ID", 0, 256), [[1, 256]], 0)
-    iota(reg("C12", 0, 12), [[1, 3], [48, 4]], 0)
-    for q in range(3):
-        iota(reg("EM", 256 * q, 256 * q + 256), [[0, 256]], 0)
-    act(reg("M", 256 * rank, 256 * rank + 256), reg("ID", 0, 256), AF.Copy)
-    for k, q in ((1, "V"), (2, "S"), (3, "V"), (4, "S")):
+    iota(reg("M16", 0, 80), [[0, 5], [1, 16]], 0)
+    iota(reg("POS", 0, 96), [[16, 3], [0, 2], [1, 16]], 0)
+    cut = min(rank + 1, 3)
+    iota(reg("TAB", 0, 256 * cut), [[256, cut], [1, 2], [2, 128]], 256 * (3 - rank))
+    iota(reg("TAB", 256 * cut, 1024), [[256, 4 - cut], [1, 2], [2, 128]], 0)
+    for k, q in zip((1, 2, 3, 4), "VSVS"):
         n = min(256, WC - 256 * k)
         if q == "V":
             ts(reg("ID", 256 * k, 256 * k + n), reg("ID", 0, n), 256.0 * k, OP.add)
         else:
             act(reg("ID", 256 * k, 256 * k + n), reg("ID", 0, n), AF.Identity, bias=256.0 * k)
+    for k in range(2):
+        fill(reg("M", 512 * k, 512 * k + 512), 0.0)
     ts(ti(0), pI, 96, OP.bitwise_and)
     ts(ti(1), pI, 31, OP.bitwise_and)
     ts(ti(2), pI, 15, OP.bitwise_and)
-    ts(reg("ti", 8, 16), reg("pI", 0, 8), 3, OP.bitwise_and)
-    ts(tf(4), ti(0), 7.0, OP.mult)
-    copy(tf(3), ti(2))
-    ts(tf(2), ti(0), 2048.0, OP.mult, -MID, OP.add)
-    tt(tf(0), tf(4), pI, OP.add)
-    copy(tf(5), ti(1))
-    ts(tf(8), ti(0), 2.0, OP.mult)
-    tt(tf(9), tf(8), ti(1), OP.add)
-    ts(tf(6), ti(1), 32.0, OP.add)
-    ts(tf(7), ti(2), 3.0, OP.mult)
-    copy(reg("UL", 0, 8), reg("ti", 8, 16))
-    fill(reg("ZB", 0, 256), 0.0)
-    fill(reg("CK", 0, 32), STEP)
-    fill(reg("C1", 0, 32), 1.0)
-    fill(reg("H", 4 * K, 512), 0.0)
-    fill(reg("E1", OWN[0] + 128, FAR), 0.0)
+    copy(reg("tf", 0, 4), reg("ti", 0, 4))
+    act(tf(4), tf(0), AF.Identity, scale=7.0, bias=tf(3))
+    act(reg("PJ", 0, 1), tf(0), AF.Identity, bias=tf(3))
+    act(reg("PJ", 1, 2), reg("PJ", 0, 1), AF.Identity, bias=32.0)
+    act(reg("PJ", 2, 3), reg("PJ", 0, 1), AF.Copy, scale=65536.0)
+    act(tf(7), tf(2), AF.Sign, scale=-1.0, bias=15.0)
+    act(tf(6), tf(7), AF.Copy, scale=BIG)
+    ts(reg("LA2", 0, 65), reg("M16", 15, 80), tf(2), OP.is_equal, BIG, OP.mult)
+    act(reg("LA1", 0, 64), reg("LA2", 1, 65), AF.Copy, scale=2.0)
+    tt(reg("LM", 0, 64), reg("LA1", 0, 64), reg("LA2", 0, 64), OP.subtract)
+    copy(reg("LM", 64, 128), reg("LM", 0, 64), "S")
+    copy(reg("LM", 128, 256), reg("LM", 0, 128), "S")
+    fill(reg("uz", 32, 512), 0.0)
+    fill(reg("C1", 0, 32), TINY)
+    fill(reg("H", 0, 512), 0.0)
+    quant("PK0", 128, 256, "H")
     for a in range(4):
-        fill(reg("PADD", 0, 1, 32 * a, 32 * a + 32), float(FAR + LC * ((a - rank - 1) % 4 % 3) - 1))
-    act(reg("GCOL", 0, 8), reg("ID", 0, 8), AF.Identity, scale=32.0, bias=tf(0))
-    act(reg("IC", 0, 16), reg("ID", 0, 16), AF.Identity, scale=16.0, bias=tf(3))
+        fill(blk("PADD", 0, 1, a), float(FAR + LC * ((a - rank - 1) % 4 % 3) - 1))
+    act(reg("GCOL", 0, 8), reg("ID", 0, 8), AF.Identity, scale=32.0, bias=tf(4))
+    for i, q in enumerate(rest):
+        act(blk("GCOL", 2 * i, 2 * i + 2, rank), blk("GCOL", 6, 8, rank), AF.Identity, bias=256.0 * (q - rank))
+    fill(blk("PB", 192, 256, rank), 0.0)
+    act(reg("IC", 0, 16), reg("ID", 0, 16), AF.Identity, scale=16.0, bias=tf(2))
     act(reg("ICS", 0, 8), reg("IC", 0, 8), AF.Identity, scale=-1.0, bias=-0.5)
     copy(reg("nbp", 0, 24), reg("nbP", 0, 24))
-    gather(reg("FRA", 0, 192), reg("ID", 0, 1024), reg("nbp", 0, 12))
-    gather(reg("FRB", 0, 192), reg("ID", 0, 1024), reg("nbp", 12, 24), "S")
-    copy(reg("FA", 0, 64), reg("FRA", 2, 192, st=3))
-    copy(reg("FA", 64, 128), reg("FRB", 2, 192, st=3))
-    copy(reg("FA", 128, 256, 0, 64), reg("FA", 0, 128, 64, 128))
-    copy(reg("FA", 128, 256, 64, 128), reg("FA", 0, 128, 0, 64))
-    for k in range(2):
-        o = 512 * k
-        gather(reg("uvt", o, o + 128), reg("uvs", 16 * k, 16 * k + 4), reg("UL", 0, 8), "S")
-        copy(reg("uvt", o + 128, o + 256), reg("uvt", o, o + 128), "S")
-        copy(reg("uvt", o + 256, o + 512), reg("uvt", o, o + 256), "S")
+    gather(reg("FR", 0, 192), reg("ID", 0, 1024), reg("nbp", 0, 12))
+    gather(reg("FR", 192, 384), reg("ID", 0, 1024), reg("nbp", 12, 24), "S")
+    copy(reg("FA", 0, 128), reg("FR", 2, 384, st=3))
+    copy(blk("FA", 128, 256, 0, 2), blk("FA", 0, 128, 2, 2))
+    copy(blk("FA", 128, 256, 2, 2), blk("FA", 0, 128, 0, 2))
     for h in range(2):
         quant("Q0", 128 * h, 128 * h + 128, "xt", 512 * h)
-    quant("UV2", 0, 128, "uvt")
-    quant("UV2", 128, 256, "uvt", 512)
+    quant("UV1", 0, 128, "uz")
     for c in range(2):
-        mm(c, "Q0", 128 * c, "UV2", 0, 128)
-    for c in range(2):
-        copy(reg("ec", c, c + 1), ps(c, 0, 1), "S")
+        mm(c, "Q0", 128 * c, "UV1", 0, 128)
+    copy(reg("ec", 0, 2), ps(0, 0, 513, st=512), "S")
     send("r_e", lambda c: (T.ec[:, 0:2], T.eld[slot(c)]), [reg("ec", 0, 2)])
     arrive("r_e", incoming, reg("eld", 0, 3))
+    for k in range(2):
+        fill(reg("UL", 8 * k, 8 * k + 8), 4 * k)
+        pick("UV2", 128 * k, 128 * k + 128, "UV1", 0, 128, reg("UL", 8 * k, 8 * k + 8))
     dma("Y", "d_q", cb("W", 0, 256), cb("Q0", 0, 256), [reg("Q0", 0, 256)], [reg("W", 0, 256)])
     dma("Y", "d_q", T.Ws[:, 0:256], T.Q0s[:, 0:256], [reg("Q0s", 0, 256)], [reg("Ws", 0, 256)])
-    dma("Y", "d_p", cb("PK0", 3 * K, PW), cb("Q0", 0, PW - 3 * K), [reg("Q0", 0, PW - 3 * K)], [reg("PK0", 3 * K, PW)])
-    dma("Y", "d_p", T["PK0s"][:, 3 * K:PW], T.Q0s[:, 0:PW - 3 * K], [reg("Q0s", 0, PW - 3 * K)], [reg("PK0s", 3 * K, PW)])
-    for c in range(8):
-        eq = reg("EQ", 256 * c, 256 * c + 256)
-        ts(eq, reg("FA", 0, 256), reg("GCOL", c, c + 1), OP.is_equal)
-        if c < 8 - SCN_S:
-            scan(reg("SC", 128 * c, 128 * c + 128), reg("EQ", 256 * c, 256 * c + 128), reg("EQ", 256 * c + 128, 256 * c + 256))
-            n = reg("SC", 128 * c + 127, 128 * c + 128)
-        else:
-            n = reg("SS", c, c + 1)
-            act(reg("SJ", 0, 256), eq, AF.Copy, accum=n)
-        act(reg("PB", 32 * c, 32 * c + 32), reg("ZB", 0, 32), AF.Sign, bias=n)
+    for c in range(6):
+        ts(reg("EQ", 256 * c, 256 * c + 256), reg("FA", 0, 256), reg("GCOL", c, c + 1), OP.is_equal)
+        scan(reg("SC", 128 * c, 128 * c + 128), reg("EQ", 256 * c, 256 * c + 128), reg("EQ", 256 * c + 128, 256 * c + 256))
+        act(reg("PB", 32 * c, 32 * c + 32), reg("H", 192, 224), AF.Sign, bias=reg("SC", 128 * c + 127, 128 * c + 128))
+        o = 192 + 32 * (c % 2)
+        act(blk("PB", o, o + 32, rest[c // 2]), blk("H", 192, 224, rank), AF.Sign, bias=blk("SC", 128 * c + 127, 128 * c + 128, rank))
     turn(reg("PR", 0, 256), reg("PB", 0, 256))
-    scan(reg("SCN", 0, 256), reg("PR", 0, 256), reg("ZB", 0, 256))
+    scan(reg("SCN", 0, 256), reg("PR", 0, 256), reg("PR", 0, 256), OP.max)
     nv = 6 - LEN_S
     for c in range(nv):
         ts(reg("LE", 256 * c, 256 * c + 256), reg("SCN", 0, 256), reg("IC", c, c + 1), OP.is_le)
@@ -342,219 +338,159 @@ def rank_program(g, core, T, topo):
     ts(reg("LST", nv, 6), reg("LS", nv, 6), -0.5, OP.mult, 127.5, OP.add)
     send("r_l", lambda c: (T.LST[:, 0:6], T.LA[:, 6 * slot(c):6 * slot(c) + 6]), [reg("LST", 0, 6)])
     arrive("r_l", incoming, reg("LA", 0, 18))
-    for d in range(4):
-        dma("Y", "d_e", T.EM[32 * d:32 * d + 1, 0:768], T.eld[0:3], [reg("eld", 0, 3)], [reg("EM", 0, 768, 32 * d, 32 * d + 1)])
     act(reg("SLf", 0, 256), reg("SCN", 0, 256), AF.Identity, bias=reg("PADD", 0, 1))
-    for q in range(4):
-        if q != rank:
-            for d in range(4):
-                dma("Y", "d_m", T.M[32 * d:32 * d + 32, 256 * q:256 * q + 256], T.SLf[32 * q:32 * q + 32, :], [reg("SLf", 0, 256, 32 * q, 32 * q + 32)], [reg("M", 256 * q, 256 * q + 256, 32 * d, 32 * d + 32)])
-    copy(reg("nbo", 0, 12), reg("nbI", 0, 12))
+    for q in rest:
+        dma("Y", "d_m", T.M[0:128:16, 256 * q:256 * q + 256], T.SLf[32 * q:32 * q + 8, :], [blk("SLf", 0, 256, q)], [reg("M", 256 * q, 256 * q + 256)])
+    for k in range(3):
+        latch(reg("LQ", 64 * k, 64 * k + 64), reg("FR", k, 192, st=3), 64)
+    ts(reg("nbK", 0, 8), reg("LQ", 15, 128, st=16), tf(6), OP.add, float(-256 * rank), OP.add)
+    ts(reg("nbK", 8, 12), reg("LQ", 143, 192, st=16), tf(6), OP.add)
     for h in range(2):
-        ts(reg("KDL", h, 24, st=2), reg("C12", 0, 12), tf(7), OP.add)
-    gather(reg("FR", 0, 192), reg("ID", 0, 1024), reg("nbo", 0, 12), "S")
-    gather(reg("PDn", 0, 256), reg("FR", 0, 192), reg("KDL", 0, 16), "S")
-    gather(reg("PDn", 256, 384), reg("FR", 0, 192), reg("KDL", 16, 24), "S")
-    turn(reg("PTn", 0, 256), reg("PDn", 0, 256))
-    turn(reg("PTn", 256, 384), reg("PDn", 256, 384))
-    ts(reg("nbK", 0, 8), reg("PTn", 0, 256, st=32), float(-256 * rank), OP.add)
-    copy(reg("nbD", 16, 24), reg("PTn", 256, 384, st=16))
-    copy(reg("nbK", 8, 12), reg("PTn", 256, 384, st=32))
-    m0, m1, n0, n1, n2, n3, n4 = [reg("Ne", 4 * i, 4 * i + 4) for i in range(7)]
-    ts(m0, reg("PTn", 256, 384, st=32), float(1024 - 256 * (rank + 1)), OP.add)
-    ts(m1, m0, 1023, OP.bitwise_and)
-    ts(n0, m0, 127, OP.bitwise_and)
-    ts(n1, m0, 7, OP.logical_shift_right, 1, OP.bitwise_and)
-    tt(n2, n0, m1, OP.add)
-    ts(n3, n1, -127.0, OP.mult)
-    tt(n4, n2, n3, OP.add)
-    copy(reg("nbe", 0, 4), n4)
+        ts(reg("nbD", h, 8, st=2), reg("LQ", 143, 192, st=16), tf(6), OP.add)
+    gather(reg("TG", 0, 64), reg("TAB", 0, 1024), reg("nbK", 8, 12), "S")
+    latch(reg("LQ", 192, 256), reg("TG", 0, 64), 64)
+    ts(reg("nbe", 0, 4), reg("LQ", 207, 256, st=16), tf(6), OP.add)
+    for d in range(4):
+        dma("Y", "d_e", T.TAB[32 * d:32 * d + 1, 0:768], T.eld[0:3], [reg("eld", 0, 3)], [reg("TAB", 0, 768, 32 * d, 32 * d + 1)])
     quant("Qb", 0, 256, "bt")
     mm(5, "UV2", 0, "Q0", 0, 256)
     mm(4, "UV2", 128, "Qb", 0, 256)
-    for b in range(2):
-        ts(reg("Ft", 64 * b, 64 * b + 64), reg("ID", 0, 64), tf(5 + b), OP.is_lt, 2.0 ** -24, OP.mult)
+    ts(reg("Ft", 0, 32), reg("ID", 0, 32), tf(1), OP.is_lt, 2.0 ** -24, OP.mult)
     copy(reg("E1", 0, 256), ps(5, 0, 256), "S")
     for a in range(4):
-        copy(reg("fb", 0, 64, 32 * a, 32 * a + 32), ps(4, 64 * a, 64 * a + 64, 32 * a, 32 * a + 32), "S")
-    act(reg("Fm", 0, 128), reg("Ft", 0, 128), AF.Identity, bias=PRED)
+        copy(blk("fb", 0, 64, a), ps(4, 64 * a, 64 * a + 64, 32 * a, 32 * a + 32), "S")
+    for b in range(2):
+        act(reg("Fm", 32 * b, 32 * b + 32), reg("Ft", 0, 32), AF.Identity, bias=PRED)
     copy(reg("Mo", 0, 256), reg("ID", 0, 256), "S")
     for k in range(2):
-        for i in range(2):
-            ts(reg("FN", 256 * k + 64 * i, 256 * k + 64 * i + 64), reg(("FRA", "FRB")[i], k, 192, st=3), float(-256 * rank), OP.add)
-        copy(reg("FN", 256 * k + 128, 256 * k + 256, 0, 64), reg("FN", 256 * k, 256 * k + 128, 64, 128))
+        ts(reg("FN", k, 256, st=2), reg("FR", k, 384, st=3), float(-256 * rank), OP.add)
+    copy(blk("FN", 256, 512, 0), blk("FN", 0, 256, 2))
     for h in range(2):
-        for k in range(3):
-            f, o = ("FN", 256 * k) if k < 2 else ("FA", 0)
-            dma("Y", "d_g", T.nbG[64 * h:64 * h + 64, 16 * k:16 * k + 16], T[f][0:64:16, o:o + 256], [reg(f, o, o + 256, 0, 64)], [reg("nbG", 16 * k, 16 * k + 16, 64 * h, 64 * h + 64)])
+        dma("Y", "d_g", T.nbG[64 * h:64 * h + 64, 0:32], T.FN[0:32:8, 0:512], [blk("FN", 0, 512, 0)], [reg("nbG", 0, 32, 64 * h, 64 * h + 64)])
     for h in range(2):
-        copy(reg("DL", h, 32, st=2), reg("IC", 0, 16))
-    iota(reg("VP", 0, 96), [[0, 2], [1, 48]], OWN[2])
-    iota(reg("OFF", 0, 96), [[-16, 3], [0, 2], [-1, 16]], 0)
-    for k in range(2):
-        ts(reg("PAYJ", k, k + 1), tf(9), 1.0 / STEP1, OP.mult, k * 32.0 / STEP1, OP.add)
-    act(reg("OFF", 96, 192), reg("OFF", 0, 96), AF.Identity, bias=reg("PAYJ", 1, 2))
-    act(reg("OFF", 0, 96), reg("OFF", 0, 96), AF.Identity, bias=reg("PAYJ", 0, 1))
-    act(reg("JB", 0, 64), reg("ID", 0, 64), AF.Identity, scale=1024.0, bias=tf(2))
-    act(reg("TB", 0, 4), reg("IC", 0, 4), AF.Identity, scale=-STEP, bias=MID)
+        dma("Y", "d_h", T.nbG[64 * h:64 * h + 64, 32:48], T.FA[0:32:8, 0:256], [blk("FA", 0, 256, 0)], [reg("nbG", 32, 48, 64 * h, 64 * h + 64)])
     for t in range(4):
         copy(reg("bbT", 256 * t, 256 * t + 256), reg("bt", t, 1024, st=4), "S")
-    for d in range(4):
-        copy(reg("LO", 0, 18, 32 * d, 32 * d + 32), reg("LA", 0, 18, 32 * rank, 32 * rank + 32))
-    pick("SND", 0, 288, "Q0", 256, reg("LO", 0, 18))
+    for d in rest:
+        copy(blk("LA", 0, 18, d), blk("LA", 0, 18, rank))
+    pick("SND", 0, 288, "Q0", 0, 256, reg("LA", 0, 18))
     ship("r_c", "SND", lambda c: LC * sources.index(c), LC, lambda c: FAR + LC * slot(c), 0, 3 * LC)
     arrive("r_c", 2 * incoming, *both("W", FAR, FAR + 3 * LC))
 
-    z0, z1, z2, EG = reg("z0", 0, 64), reg("z1", 0, 64), reg("z2", 0, 64), reg("EG", 0, 64)
+    z0, z1, z2, EG, zr = reg("z0", 0, 64), reg("z1", 0, 64), reg("z2", 0, 64), reg("EG", 0, 64), reg("Zc", 256, 320)
     M = reg("M", 0, 1024)
     Mo = reg("Mo", 0, 256)
     C005 = 13421773.0 * 2.0 ** -28
 
-    def payload01():
-        gather(reg("PC", 0, 128), Mo, reg("nbK", 0, 8), "S")
-        act(reg("zK", 0, 64), reg("PC", 64, 128), AF.Identity, scale=512.0, bias=-MID)
-        tt(reg("PAB", 0, 64), reg("zK", 0, 64), reg("PC", 0, 64), OP.add)
-        turn(reg("PAYT", 0, 64), reg("PAB", 0, 64))
+    def at_places(oh, th, xh, o, pay):
+        for b in range(2):
+            ts(reg(oh, o + 96 * b, o + 96 * b + 96), reg("POS", 0, 96), reg("RS", 128 * b + 127, 128 * b + 128), OP.is_equal, pay[b], OP.mult)
+            turn(reg(th, o + b, o + 192, st=2), reg(oh, o + 96 * b, o + 96 * b + 96))
+        for c in range(o, o + 192, 64):
+            scan(blk(xh, c, c + 64, 0, 2), blk(th, c, c + 64, 0, 2), blk(th, c, c + 64, 2, 2))
 
-    def payload2():
-        gather(reg("PC", 128, 192), M, reg("nbK", 8, 12), "S")
-        tt(reg("PAB", 64, 128), reg("PC", 128, 192), reg("JB", 0, 64), OP.add)
-        turn(reg("PAYT", 64, 128), reg("PAB", 64, 128))
+    def joined(out, c0, xh, o):
+        for d in range(2):
+            tt(blk(out, c0, c0 + 3, d), blk(xh, o + 63, o + 192, 0, st=64), blk(xh, o + 63, o + 192, 1, st=64), OP.add)
 
+    def to_list(out, c0, src, s0, n):
+        for d in (0, 2):
+            copy(blk(out, c0, c0 + n, d, 2), blk(src, s0, s0 + n, 0, 2))
+
+    quant("Qa", 0, 256, "at")
+    quant("Qa", 256, 512, "at", 1024)
     quant("Qw", 0, 128, "wt")
     mm(5, "Qw", 0, "Q0", 0, 256)
     copy(reg("ys", 0, 256), ps(5, 0, 256), "S")
     for t in range(R):
         SL, SR = "SL%d" % t, "SR%d" % t
-        PO, J, nf = reg("PO", 10 * t, 10 * t + 9), reg("J", 4 * t, 4 * t + 3), reg("nf", 3 * t, 3 * t + 3)
-        nk, Jn = (2, reg("Ji", 0, 3)) if t == 0 else (1, reg("Dj", 0, 3))
+        J = reg("J", 4 * t, 4 * t + 3)
         wend, w0 = WEND[t], OWN[t]
         if t == 0:
-            gather(EG, reg("E1", 0, 256), reg("nbK", 0, 4))
+            gather(EG, reg("E1", 0, 256), reg("nbK", 0, 4), "S")
             tt_by(z0, reg("E1", 0, 256), reg("nbK", 4, 8), EG, OP.add)
-            tt_by(z1, reg("EM", 0, 768), reg("nbe", 0, 4), z0, OP.add)
-            payload01()
-            payload2()
+            tt_by(z1, reg("TAB", 0, 768), reg("nbe", 0, 4), z0, OP.add)
+            for b in range(2):
+                act(reg("zK", 32 * b, 32 * b + 32), reg("FR", 1 + 96 * b, 96 * b + 96, st=3), AF.Identity, scale=256.0, bias=65536.0 * 32 * b - 257.0 * 256 * rank)
+            tt(reg("PAB", 0, 64), reg("zK", 0, 64), reg("FR", 0, 192, st=3), OP.add)
+            turn(reg("PAYT", 0, 64), reg("PAB", 0, 64))
+            ts(reg("PAY", 0, 2), reg("PAYT", 0, 64, st=32), reg("PJ", 2, 3), OP.add)
+            act(reg("PC", 0, 64), M, AF.Identity, bias=float(-FAR), by=reg("nbK", 8, 12))
+            turn(reg("PAYT", 64, 128), reg("PC", 0, 64))
         else:
             a0 = ARR[t - 1]
             mm(6, "UV2", 0, "W", a0, 3 * K)
             copy(reg("E1", a0, a0 + 3 * K), ps(6, 0, 3 * K))
-            tt_by(z1, reg("E1", FAR, wend), reg("EO", 8, 12), z0, OP.add)
+            tt_by(z1, reg("E1", FAR, wend), reg("EO", 0, 4), z0, OP.add)
         tt(z2, z1, reg("fb", 0, 64), OP.subtract)
-        act(reg("zr", 0, 64), z2, AF.Abs, bias=TINY)
-        turn(reg("ZT", 0, 64), reg("zr", 0, 64))
-        zr, zs = "zr", "z2"
         if t == 0:
+            turn(reg("zB", 0, 64), z2)
             for b in range(2):
-                ts(reg("zB", 32 * b, 32 * b + 32), reg("C1", 0, 32), reg("ZT", 32 * b, 32 * b + 1), OP.mult)
-            turn(reg("zr0", 0, 64), reg("zB", 0, 64))
-            zr = zs = "zr0"
-        for b in range(2):
-            tt(reg("Zc", 256 * b, 256 * b + 64), reg(zr, 0, 64), reg("Fm", 64 * b, 64 * b + 64), OP.mult)
-        for q, d, s, w, x in (("S", 0, 2, 2, 2), ("S", 2, 0, 2, 2), ("S", 0, 1, 1, 1), ("S", 1, 0, 1, 1), ("S", 2, 3, 1, 1), ("S", 3, 2, 1, 1), ("S", 0, 3, 1, 3), ("V", 3, 0, 1, 3), ("V", 1, 2, 1, 3), ("S", 2, 1, 1, 3)):
-            o = reg("Zc", 64 * x, 64 * x + 64, 32 * d, 32 * d + 32 * w)
-            i = reg(zs if q == "S" else zr, 0, 64, 32 * s, 32 * s + 32 * w)
+                act(reg("ZT", 32 * b, 32 * b + 32), reg("C1", 0, 32), AF.Abs, bias=reg("zB", 32 * b, 32 * b + 1))
+            turn(zr, reg("ZT", 0, 64))
+        else:
+            act(zr, z2, AF.Abs, bias=TINY)
+            turn(reg("ZT", 0, 64), zr)
+        tt(reg("Zc", 192, 256), zr, reg("Fm", 0, 64), OP.mult)
+        moves = [(0, 2, 2, 0), (2, 0, 2, 0), (0, 1, 1, 1), (1, 0, 1, 1), (2, 3, 1, 1), (3, 2, 1, 1), (0, 3, 1, 2), (2, 1, 1, 2), (3, 0, 1, 2), (1, 2, 1, 2)]
+        for n, (d, s, w, x) in enumerate(moves):
+            o = blk("Zc", 64 * x, 64 * x + 64, d, w)
             f = PRED if s > d else 1.0
-            if q == "S":
+            if n < len(moves) - VX:
                 if t == 0:
-                    act(o, i, AF.Copy, scale=f)
+                    act(o, blk("Zc", 256, 320, s, w), AF.Copy, scale=f)
                 else:
-                    act(o, i, AF.Abs, scale=f, bias=TINY * f)
+                    act(o, blk("z2", 0, 64, s, w), AF.Abs, scale=f, bias=TINY * f)
             elif s > d:
-                ts(o, i, f, OP.mult)
+                ts(o, blk("Zc", 256, 320, s, w), f, OP.mult)
             else:
-                copy(o, i)
-        ts(reg("ZN", 0, 1), reg("ZT", 32, 33), -UP, OP.mult)
-        ts(reg("MK", 256, 256 + VPART), reg("Zc", 64, 64 + VPART), reg("ZT", 32, 33), OP.is_ge, 1.0, OP.subtract)
-        act(reg("MK", 256 + VPART, 512), reg("Zc", 64 + VPART, 320), AF.Sign, scale=UP, bias=reg("ZN", 0, 1))
-        for h in range(2):
-            ts(reg("MK", 128 * h, 128 * h + 128), reg("Zc", 128 * h, 128 * h + 128), reg("ZT", 0, 1), OP.is_ge)
-        act(reg("SJ", 0, 256), reg("MK", 256, 512), AF.Sign, bias=1.0, accum=reg("SS", 0, 1))
-        scan(reg("RS", 0, 128), reg("MK", 0, 128), reg("MK", 128, 256))
+                copy(o, blk("Zc", 256, 320, s, w))
+        ts(reg("MK", 224, 256), reg("Zc", 288, 320), reg("ZT", 0, 1), OP.is_gt)
+        ts(reg("MK", 448, 512), reg("Zc", 224, 288), reg("ZT", 32, 33), OP.is_ge)
+        for b in range(2):
+            n = 224 - 32 * b
+            ts(reg("MK", 256 * b, 256 * b + n), reg("Zc", 0, n), reg("ZT", 32 * b, 32 * b + 1), OP.is_ge)
+            scan(reg("RS", 128 * b, 128 * b + 128), reg("MK", 256 * b, 256 * b + 128), reg("MK", 256 * b + 128, 256 * b + 256))
         if t == 0:
-            for k in range(2):
-                o = 64 * k
-                ts(reg("KB", o, o + 32), reg("CK", 0, 32), reg("RS", 127, 128), OP.mult, reg("PAYT", o, o + 1), OP.add)
-                act(reg("KB", o + 32, o + 64), reg("CK", 0, 32), AF.Identity, scale=reg("SS", 0, 1), bias=reg("PAYT", o + 32, o + 33))
-            turn(reg("KEY", 0, 128), reg("KB", 0, 128))
-            for c in range(3):
-                o, tb = reg("DK", 128 * c, 128 * c + 128), reg("TB", c, c + 1)
-                if c == 2:
-                    ts(o, reg("KEY", 0, 128), tb, OP.add)
-                else:
-                    act(o, reg("KEY", 0, 128), AF.Identity, bias=tb)
-            for c in range(3):
-                for k in range(2):
-                    least(reg("R0", 3 * k + c, 3 * k + c + 1), reg("DK", 128 * c + 64 * k, 128 * c + 64 * k + 64))
+            at_places("OF", "TF", "XF", 0, [reg("PAY", b, b + 1) for b in range(2)])
+            joined("Ri", 0, "XF", 0)
+            ts(blk("Di", 0, 3, 0, 2), blk("Ri", 0, 3, 0, 2), 255, OP.bitwise_and)
+            ts(blk("Di", 3, 6, 0, 2), blk("Ri", 0, 3, 0, 2), 8, OP.logical_shift_right, 255, OP.bitwise_and)
+            ts(blk("Di", 6, 9, 0, 2), blk("Ri", 0, 3, 0, 2), 16, OP.logical_shift_right)
+            to_list("PO", 0, "Di", 0, 9)
+            J = reg("PO", 6, 9)
+            copy(blk("YJ", 0, 3, 0), blk("Di", 6, 9, 0))
+            pick("PK0", K, 3 * K, "Q0", 0, 256, reg("PO", 0, 6))
+            at_places("OF", "TF", "XF", 192, [reg("PAYT", 64 + 32 * b, 65 + 32 * b) for b in range(2)])
+            joined("Ri", 3, "XF", 192)
+            to_list("PF", 0, "Ri", 3, 3)
+            pick("PK0", 0, K, "W", FAR, wend, reg("PF", 0, 3))
         else:
-            for c in range(3):
-                o = 64 * c
-                ts(reg("KB", o, o + 32), reg("OFF", 32 * c, 32 * c + 32), reg("RS", 127, 128), OP.add)
-                act(reg("KB", o + 32, o + 64), reg("OFF", 96 + 32 * c, 128 + 32 * c), AF.Identity, bias=reg("SS", 0, 1))
-            for c in range(3):
-                o = 64 * c
-                turn(reg("KEY", o, o + 64), reg("KB", o, o + 64))
-                least(reg("R0", c, c + 1), reg("KEY", o, o + 64))
-        n3 = 3 * nk
-        for d in range(2):
-            tt(reg("R1", 0, n3, 64 * d, 64 * d + 64), reg("R0", 0, n3, 64 * d, 64 * d + 64), reg("R0", 0, n3, 64 - 64 * d, 128 - 64 * d), OP.min)
-        Rd = "Ri" if t == 0 else "Rf"
-        for d in range(4):
-            s = d ^ 1
-            tt(reg(Rd, 0, n3, 32 * d, 32 * d + 32), reg("R1", 0, n3, 32 * d, 32 * d + 32), reg("R1", 0, n3, 32 * s, 32 * s + 32), OP.min)
-        if t == 0:
-            ts(reg("Di", 0, 3), reg("Ri", 0, 3), 511, OP.bitwise_and)
-            ts(reg("Di", 3, 6), reg("Ri", 0, 3), 9, OP.logical_shift_right)
-            ts(reg("Di", 6, 9), reg("Ri", 3, 6), 1023, OP.bitwise_and)
-            copy(PO, reg("Di", 0, 9))
-            pick("PK0", 0, 144, "W", wend, PO)
-            ts(Jn, reg("Ri", 3, 6), 10, OP.logical_shift_right)
-            copy(J, Jn)
-        else:
-            ts(J, reg("Rf", 0, 3), STEP1, OP.mult)
-            ts(Jn, reg("Rf", 0, 3), STEP1, OP.mult)
+            at_places("OH", "TH", "XH", 0, [reg("PJ", b, b + 1) for b in range(2)])
+            joined("YJ", 3 * t, "XH", 0)
+            to_list("J", 4 * t, "YJ", 3 * t, 3)
         if t < 2:
-            ts(reg(SL, 0, 3), Jn, float(256 * rank), OP.add)
+            ts(reg(SL, 0, 3), J, float(256 * rank), OP.add)
             send("r_s%d" % t, lambda c, SL=SL, SR=SR: (T[SL][:, 0:3], T[SR][:, 3 * slot(c):3 * slot(c) + 3]), [reg(SL, 0, 3)])
             arrive("r_s%d" % t, incoming, reg(SR, 0, 9))
-        if t < 2:
-            scatter(Mo, J, reg("ID", w0, w0 + K))
-        else:
-            ts(reg("Dj", 8, 11), Jn, 240, OP.bitwise_and)
-            tt(reg("Dj", 4, 7), Jn, reg("Dj", 8, 11), OP.add)
-            copy(reg("JD", 0, 3), reg("Dj", 4, 7))
-            ts(reg("JD", 3, 6), reg("Dj", 4, 7), 16.0, OP.add)
-            scatter(reg("MoD", 0, 512), reg("JD", 0, 6), reg("VP", 0, 96))
-            for h in range(4):
-                turn(reg("FT", 128 * h, 128 * h + 128), reg("MoD", 128 * h, 128 * h + 128))
-            for h in range(2):
-                copy(reg("FO", 8 * h, 8 * h + 8), reg("FT", 256 * h, 256 * h + 256, st=32))
+        scatter(Mo, J, reg("ID", w0, w0 + K))
+        if t == 2:
+            latch(reg("FT", 0, 256), Mo, 256)
+            ts(reg("FO", 0, 16), reg("FT", 15, 256, st=16), tf(6), OP.add)
+        for b in range(4):
+            gather(reg("G4", K * b, K * b + K), reg("bbT", 256 * b, 256 * b + 256), J, "S")
         if t == 0:
-            quant("Qa", 0, 256, "at")
-            quant("Qa", 256, 512, "at", 1024)
-            for b in range(4 - INP):
-                mm(b, "Qa", 128 * b, "PK0", 0, 3 * K)
-            for b in range(4 - INP, 4):
-                for k in range(3):
-                    mm(b, "Qa", 128 * b, "PK0", K * k, 128, k == 0, k == 2)
+            for k in range(3):
+                for b in range(4):
+                    mm(b, "Qa", 128 * b, "PK0", K * ((k + 1) % 3), 128, k == 0, k == 2)
             for b in range(4):
-                s0, s1, s2, s3 = [reg("SU", 192 * k + K * b, 192 * k + K * b + K) for k in range(4)]
-                if b < 4 - INP:
-                    copy(s0, ps(b, 0, K), "S")
-                    tt(s1, ps(b, K, 2 * K), s0, OP.add)
-                    tt(s2, ps(b, 2 * K, 3 * K), s1, OP.add)
-                else:
-                    s2 = ps(b, 0, K)
-                act(s3, s2, AF.Copy, scale=C005)
-                tt_by(reg("H", b, 4 * K, st=4), reg("bbT", 256 * b, 256 * b + 256), J, s3, OP.add)
-        else:
-            for b in range(4):
-                gather(reg("G4", K * b, K * b + K), reg("bbT", 256 * b, 256 * b + 256), J, "S")
-            for b in range(4):
-                tt_by(reg("H", b, 4 * K, st=4), reg("ST", 256 * b, 256 * b + 256), J, reg("G4", K * b, K * b + K), OP.add)
-        if t == 0:
+                act(reg("SU", K * b, K * b + K), ps(b, 0, K), AF.Copy, scale=C005)
+                tt(reg("H", b, 4 * K, st=4), reg("SU", K * b, K * b + K), reg("G4", K * b, K * b + K), OP.add)
             mm(7, "UV2", 0, "W", FAR, 3 * LC)
             copy(reg("E1", FAR, FAR + 3 * LC), ps(7, 0, 3 * LC), "S")
+        else:
+            for b in range(4):
+                tt_by(reg("H", b, 4 * K, st=4), reg("ST", 256 * b, 256 * b + 256), J, reg("G4", K * b, K * b + K), OP.add)
         quant("W", w0, w0 + 128, "H")
         if t < 2:
             ship("r_n%d" % t, "W", lambda c, w0=w0: w0, K, lambda c, t=t: ARR[t] + K * slot(c), w0, w0 + K)
@@ -564,41 +500,35 @@ def rank_program(g, core, T, topo):
             mm(7, "UV2", 0, "W", w0, 128)
             copy(reg("en", K * t, K * t + K), ps(7, 0, K), "S")
             scatter(reg("E1", 0, 256), J, reg("en", K * t, K * t + K))
-            gather(EG, reg("E1", 0, 256), reg("nbK", 0, 4))
+            gather(EG, reg("E1", 0, 256), reg("nbK", 0, 4), "S")
             tt_by(z0, reg("E1", 0, 256), reg("nbK", 4, 8), EG, OP.add)
-            w = 256 // NP
             for k in range(2):
                 gather(reg("LRo", 256 * k, 256 * k + 256), Mo, reg("nbG", 16 * k, 16 * k + 16), "S")
-                as_list("d_l%d" % (3 * t + k), "LIo", 32 * t + 16 * k, "LRo", 256 * k)
+            dma("Y", "d_l%d" % (2 * t), T.LIo[:, 32 * t:32 * t + 32], T.LRo[0:128:16, 0:512], [reg("LRo", 0, 512)], [reg("LIo", 32 * t, 32 * t + 32)])
+            copy(reg("Lu", 48 * t, 48 * t + 32), reg("LIo", 32 * t, 32 * t + 32))
+            for k in range(2):
                 o = 48 * t + 16 * k
-                copy(reg("Lu", o, o + 16), reg("LIo", 32 * t + 16 * k, 32 * t + 16 * k + 16))
-                for h in range(NP):
-                    pick(PA, 256 * k + w * h, 256 * k + w * h + w, "W", w0 + K, reg("Lu", o + w // 16 * h, o + w // 16 * (h + 1)))
+                pick(PA, 256 * k, 256 * k + 256, "W", 0, w0 + K, reg("Lu", o, o + 16))
                 for b in range(4):
                     mm(b, "Qa", 128 * b, PA, 256 * k, 256, k == 0, False)
             scatter(M, reg(SR, 0, 9), reg("ID", ARR[t], ARR[t] + 3 * K))
-            gather(reg("PD", 256, 384), M, reg("nbD", 16, 24), "S")
-            turn(reg("PT", 256, 384), reg("PD", 256, 384))
-            ts(reg("EO", 8, 12), reg("PT", 256, 384, st=32), float(-FAR), OP.add)
+            gather(reg("PD", 0, 128), M, reg("nbD", 0, 8), "S")
+            turn(reg("PT", 0, 128), reg("PD", 0, 128))
+            ts(reg("EO", 0, 4), reg("PT", 0, 128, st=32), float(-FAR), OP.add)
             gather(reg("LRf", 0, 256), M, reg("nbG", 32, 48), "S")
-            as_list("d_l%d" % (3 * t + 2), "LIf", 16 * t, "LRf", 0)
+            dma("Y", "d_l%d" % (2 * t + 1), T.LIf[:, 16 * t:16 * t + 16], T.LRf[0:128:16, 0:256], [reg("LRf", 0, 256)], [reg("LIf", 16 * t, 16 * t + 16)])
             o = 48 * t + 32
-            copy(reg("Lu", o, o + 16), reg("LIf", 16 * t, 16 * t + 16))
-            for h in range(NP):
-                pick(PA, 512 + w * h, 512 + w * h + w, "W", WEND[u], reg("Lu", o + w // 16 * h, o + w // 16 * (h + 1)))
+            ts(reg("Lu", o, o + 16), reg("LIf", 16 * t, 16 * t + 16), float(-FAR), OP.add)
+            pick(PA, 512, 768, "W", FAR, WEND[u], reg("Lu", o, o + 16))
             for b in range(4):
                 mm(b, "Qa", 128 * b, PA, 512, 256, False, True)
             for b in range(4):
                 act(reg("ST", 256 * b, 256 * b + 256), ps(b, 0, 256), AF.Copy, scale=C005)
         else:
             for h in range(2):
-                pick("FIN", 128 * h, 128 * h + 128, "W", WC, reg("FO", 8 * h, 8 * h + 8))
-        copy(nf, Jn)
+                pick("FIN", 128 * h, 128 * h + 128, "W", 0, WC, reg("FO", 8 * h, 8 * h + 8))
         for c in range(3):
-            dma("Y", "d_nd", T.nd[t:t + 1, 16 * c:16 * c + 16], T.nf[0:16, 3 * t + c:3 * t + c + 1], [nf], [])
-        if t == 1:
-            for h in range(4):
-                gather(reg("MoD", 128 * h, 128 * h + 128), Mo, reg("DL", 8 * h, 8 * h + 8), "S")
+            dma("Y", "d_nd", T.nd[t:t + 1, 16 * c:16 * c + 16], T.YJ[0:16, 3 * t + c:3 * t + c + 1], [blk("YJ", 3 * t, 3 * t + 3, 0)], [])
         mm(4, "Qw", 0, "W", w0, 128)
         copy(reg("yn", K * t, K * t + K), ps(4, 0, K), "S")
         scatter(reg("ys", 0, 256), J, reg("yn", K * t, K * t + K))
@@ -606,10 +536,9 @@ def rank_program(g, core, T, topo):
     dma("Y", "d_out", T.oc[:, 0:1024], cb("FIN", 0, 256), [reg("FIN", 0, 256)], [])
     for k in range(4):
         dma("YYSS"[k], "d_out", T.osc[4 * k:4 * k + 4, 0:256], T.FINs[32 * k:32 * k + 4, 0:256], [reg("FINs", 0, 256)], [])
-    for h in range(2):
-        dma("YS"[h], "d_out", T.y[:, 128 * h:128 * h + 128], T.ys[:, 128 * h:128 * h + 128], [reg("ys", 128 * h, 128 * h + 128)], [])
-    for i in ORDER:
-        calls[i]()
-    for s in ("v", "s", "p", "gq", "d_q", "d_g", "d_nd", "d_out", "loc"):
+    dma("S", "d_out", T.y[:], T.ys[:], [reg("ys", 0, 256)], [])
+    for i in ORDER or range(len(calls)):
+        issue(*calls[i])
+    for s in ("v", "s", "p", "gq", "d_q", "d_g", "d_h", "d_nd", "d_out", "loc"):
         if know["G"].get(s, 0) < count[s]:
             g.wait_ge(T.sem[s], count[s])

from concourse.bass import DstId, RemoteDMATransfer
from concourse.mybir import AluOpType as OP, ActivationFunctionType as AF, dt

P, K, R, LC = 256, 48, 3, 96
OWN = [P, P + K]
FAR = 448
ARR = [FAR + 3 * LC, FAR + 3 * LC + 3 * K]
OWN.append(ARR[1] + 3 * K)
WEND = [ARR[0], ARR[1], OWN[2]]
WC = OWN[2] + 128
TINY = 2.0 ** -122
PRED = 1.0 - 2.0 ** -24
BIG = 2048.0
LEN_S = 3
VX = 2
ORDER = [int(_i) for _i in """
14 12 19 46 6 3 11 2 21 13 10 7 5 48 8 1 33 9 4 0 15 18 20 31 16 58 53 32 78 47 51 34 30 24 39 59 143 36 50 35 27 54 60 40 149 41 56 29 42 23 26 25 150 28 57 151 67 75 43 68 61 69 44 37 62 63 71 52 79 55 70 64 128 72 66 180 49 45 65 159 73 76 99 179 91 74 158 38 157 160 95 17 87 80 103 77 92 100 88 130 104 131 101 96 102 141 126 133 127 83 106 152 93 89 84 97 134 98 140 105 94 90 85 86 129 144 142 107 161 181 108 135 132 111 115 109 113 112 116 173 182 137 114 176 138 110 139 117 136 174 177 147 146 118 148 145 119 175 178 120 122 153 186 22 187 125 171 124 82 123 81 188 189 172 162 121 190 183 191 200 192 202 193 164 194 195 163 165 198 201 199 203 197 166 196 167 206 184 204 168 207 169 205 210 154 208 211 209 155 214 156 212 213 185 215 216 217 219 218 225 220 221 227 238 223 224 241 239 245 170 228 244 226 249 278 230 246 231 229 250 233 277 232 253 279 240 235 248 234 252 236 222 237 247 293 242 251 243 310 254 257 256 258 255 264 266 259 262 265 260 294 263 261 267 268 280 297 295 281 269 272 313 270 298 273 282 274 314 296 283 275 315 288 287 284 276 285 271 316 290 317 291 299 318 286 301 319 300 292 320 328 329 324 332 325 326 321 304 330 322 323 327 331 333 334 303 335 308 289 337 336 307 302 338 339 341 340 305 342 345 306 343 344 309 346 347 348 349 350 353 354 356 351 355 358 357 360 371 359 361 372 362 352 387 363 407 366 373 364 408 367 388 368 409 389 369 391 390 374 370 365 375 376 410 392 405 312 382 406 411 379 412 413 378 381 377 414 417 420 380 423 421 424 415 425 422 416 418 386 419 426 393 427 428 384 394 395 385 429 431 399 430 432 433 398 435 434 403 436 437 397 438 439 440 402 383 441 401 443 460 396 462 461 442 444 404 311 449 450 447 448 453 400 454 445 452 451 446 455 458 463 457 456 464 459 466 465 468 467 471 470 469
""".split()]

BUF = {
    "float32": "ID:%d Fm:64 Ft:32 FR:384 SLf:256 LJ:768 Mo:256 LRo:512 LRf:256 LIo:64 LIf:32 en:96 G4:192 ST:1024 M:1024 ec:2 TAB:1024 E1:%d fb:64 PC:64 PAB:64 PAYT:128 LQ:256 TG:64 PD:128 PT:128 EG:64 zK:64 z0:64 z1:64 z2:64 ZT:64 zB:64 Zc:320 OF:384 TF:384 XF:384 RS:256 YJ:9 SU:192 FT:256 ys:256 yn:144" % (WC, OWN[2]),
    "bfloat16": "xt:1024 bt:1024 at:2048 wt:512 uz:512 bbT:1024 EQ:1536 SC:768 PB:256 PR:256 SCN:256 LE:1536 LC2:768 MK:512 H:512 POS:96 OH:192 TH:192 XH:192 M16:80 LM:256 LA1:64 LA2:66",
    "int32": "ti:4 nbP:24 Ri:6 Di:9",
    "uint16": "UL:16 FN:512 nbG:48 Lu:96 nbp:24 nbe:4 nbD:8 nbK:12 FA:256 LST:6 LA:18 EO:4 PO:10 PF:4 J:12 SL0:4 SL1:4 SR0:9 SR1:9 FO:16",
}
SMALL = "tf:12 GCOL:8 IC:16 ICS:8 C1:32 PADD:4 LS:8 PAY:4 PJ:4"
PART = {}
_n = 0
for _b in SMALL.split():
    PART[_b.split(":")[0]] = _n
    _n += int(_b.split(":")[1])
QBUF = "Q0:256 Qb:256 Qa:512 Qw:128 UV1:128 UV2:256 SND:288 W:%d PK0:256 PA1:768 PA2:768 FIN:256" % WC
SCRATCH = {"eld": ("dram", [3, 128, 2], "float32"), "ps": ("psum", [128, 4096], "float32"), "KC": ("sbuf", [128, _n], "float32")}
for _d, _s in BUF.items():
    for _b in _s.split():
        SCRATCH[_b.split(":")[0]] = ("sbuf", [128, int(_b.split(":")[1])], _d)
for _b in QBUF.split():
    SCRATCH[_b.split(":")[0]] = ("sbuf", [128, int(_b.split(":")[1])], "float8_e4m3fn_x4")
    SCRATCH[_b.split(":")[0] + "s"] = ("sbuf", [128, int(_b.split(":")[1])], "uint8")
SEMAPHORES = "v s p gq d_nb d_x d_y d_u d_v d_bb d_a d_w d_q d_m d_e d_nd d_out d_g d_h d_l0 d_l1 d_l2 d_l3 r_e r_l r_c r_s0 r_s1 r_n0 r_n1 loc".split()


def rank_program(g, core, T, topo):
    rank = T.rank_of(core)
    if rank is None:
        return
    V, S, PE, Y = g.vector, g.scalar, g.tensor, g.sync
    queue = {"V": V, "S": S, "P": PE, "G": g, "Y": Y}
    sem_of = {"V": "v", "S": "s", "P": "p", "G": "gq"}
    count = {s: 0 for s in SEMAPHORES}
    total = {s: 0 for s in SEMAPHORES}
    know = {q: {} for q in queue}
    snaps, touched, calls, across = {}, {}, [], [0]

    def reg(name, c0, c1, p0=0, p1=128, st=1):
        if name in PART:
            return ("KC", p0, p1, c0 + PART[name], c1 + PART[name], st)
        return (name, p0, p1, c0, c1, st)

    def ap(r):
        n, p0, p1, c0, c1, st = r
        return T[n][p0:p1, c0:c1:st] if st > 1 else T[n][p0:p1, c0:c1]

    def meet(a, b):
        if a[0] == "ps":
            return a[3] // 512 <= (b[4] - 1) // 512 and b[3] // 512 <= (a[4] - 1) // 512
        if a[2] <= b[1] or b[2] <= a[1] or a[4] <= b[3] or b[4] <= a[3]:
            return False
        return not (a[5] == b[5] > 1 and a[3] % a[5] != b[3] % b[5])

    def order(q, reads, writes, acc):
        want = {}
        for r, w in [(r, False) for r in reads] + [(r, True) for r in writes]:
            for (o, ow, oq, sem, val) in touched.get(r[0], []):
                if meet(r, o) and not (acc and oq == q and r[0] == "ps") and (ow or ((w or r[0] == "ps") and oq != q)):
                    if know[q].get(sem, 0) < val:
                        want[sem] = max(want.get(sem, 0), val)
        for s in sorted(want):
            if any(o != s and snaps.get((o, want[o]), {}).get(s, 0) >= want[s] for o in want):
                del want[s]
        for s, val in want.items():
            queue[q].wait_ge(T.sem[s], val)
            know[q][s] = max(know[q].get(s, 0), val)
            for k, x in snaps.get((s, val), {}).items():
                know[q][k] = max(know[q].get(k, 0), x)

    def note(reads, writes, q, sem, val):
        for r in reads:
            touched.setdefault(r[0], []).append((r, False, q, sem, val))
        for r in writes:
            touched.setdefault(r[0], []).append((r, True, q, sem, val))

    def issue(kind, q, s, reads, writes, x, fn):
        if kind == "far":
            return note([], writes, "far", s, x)
        order(q, reads, writes, x is True)
        if q == "V" and x is False and know[q].get(s, 0) < across[0]:
            V.wait_ge(T.sem[s], across[0])
            know[q][s] = across[0]
        if kind == "send":
            fn()
        elif kind == "dma":
            count[s] += 16
            fn().then_inc(T.sem[s], 16)
            note(reads, writes, "dma", s, total[s])
        else:
            count[s] += 1
            fn().then_inc(T.sem[s], 1)
            snaps[(s, count[s])] = dict(know[q])
            note(reads, writes, q, s, count[s])
            if x == "across":
                across[0] = count[s]

    def op(q, fn, reads, writes, mark=False):
        calls.append(("op", q, sem_of[q], reads, writes, mark, fn))

    def dma(q, sem, out, in_, reads, writes):
        total[sem] += 16
        calls.append(("dma", q, sem, reads, writes, False, lambda: queue[q].dma_start(out, in_)))

    def arrive(sem, n, *writes):
        calls.append(("far", "", sem, [], list(writes), n, None))

    def sc(x):
        return ap(x) if isinstance(x, tuple) else x

    def act(out, in_, f, bias=None, scale=None, accum=None, by=None):
        kw = {}
        if bias is not None: kw["bias"] = sc(bias)
        if scale is not None: kw["scale"] = sc(scale)
        if accum is not None: kw["accum_out"] = ap(accum)
        op("S", lambda: S.activation(ap(out), ap(in_).indirect(ap(by)) if by else ap(in_), f, **kw), [in_] + [x for x in (bias, scale, by) if isinstance(x, tuple)], [out] + ([accum] if accum else []))

    def copy(out, in_, q="V"):
        if q == "V":
            op("V", lambda: V.tensor_copy(ap(out), ap(in_)), [in_], [out])
        else:
            act(out, in_, AF.Copy)

    def ts(out, in_, s1, op0, s2=None, op1=None):
        rd = [in_] + [x for x in (s1, s2) if isinstance(x, tuple)]
        if op1 is None:
            op("V", lambda: V.tensor_scalar(ap(out), ap(in_), sc(s1), None, op0), rd, [out])
        else:
            op("V", lambda: V.tensor_scalar(ap(out), ap(in_), sc(s1), sc(s2), op0, op1), rd, [out])

    def tt(out, a, b, o):
        op("V", lambda: V.tensor_tensor(ap(out), ap(a), ap(b), o), [a, b], [out], a[1] != b[1] and "across")

    def tt_by(out, win, off, b, o):
        op("V", lambda: V.tensor_tensor(ap(out), ap(win).indirect(ap(off)), ap(b), o), [win, off, b], [out])

    def scan(out, a, b, o=OP.add):
        op("V", lambda: V.tensor_tensor_scan(ap(out), ap(a), ap(b), 0.0, OP.add, o), [a, b], [out], a[1] != b[1] and "across")

    def latch(out, row, n):
        scan(out, reg("LM", 0, n), row, OP.min)

    def turn(out, in_):
        op("V", lambda: V.transpose(ap(out), ap(in_)), [in_], [out], "turn")

    def fill(out, x):
        op("V", lambda: V.memset(ap(out), x), [], [out])

    def iota(out, pattern, base, mult=0):
        if SCRATCH[out[0]][2] == "int32":
            op("G", lambda: g.iota(ap(out), pattern, base, mult), [], [out])
        else:
            op("G", lambda: g.iota(ap(out), pattern, base, mult, allow_small_or_imprecise_dtypes=True), [], [out])

    def gather(out, win, off, q="V"):
        if q == "V":
            op("V", lambda: V.tensor_copy(ap(out), ap(win).indirect(ap(off))), [win, off], [out])
        else:
            act(out, win, AF.Copy, by=off)

    def scatter(win, off, in_):
        op("V", lambda: V.tensor_copy(ap(win).indirect(ap(off)), ap(in_)), [in_, off], [win])

    def pick(dst, c0, c1, src, w0, w1, off):
        a, b = reg(dst, c0, c1), reg(src, w0, w1)
        op("V", lambda: V.tensor_copy(ap(a).bitcast(dt.uint32), ap(b).bitcast(dt.uint32).indirect(ap(off))), [b, off], [a])
        gather(reg(dst + "s", c0, c1), reg(src + "s", w0, w1), off, "S")

    def both(q, c0, c1):
        return [reg(q, c0, c1), reg(q + "s", c0, c1)]

    def quant(q, c0, c1, t, e0=0):
        e1 = e0 + 4 * (c1 - c0)
        op("V", lambda: V.quantize_mx(T[q][:, c0:c1], T[q + "s"][:, c0:c1], T[t][:, e0:e1]), [reg(t, e0, e1)], both(q, c0, c1))

    def mm(bank, a, a0, b, b0, n, start=True, stop=True):
        o = reg("ps", 512 * bank, 512 * bank + n)
        op("P", lambda: PE.matmul_mx(ap(o), T[a][:, a0:a0 + 128], T[a + "s"][:, a0:a0 + 128], T[b][:, b0:b0 + n], T[b + "s"][:, b0:b0 + n], start, stop), both(a, a0, a0 + 128) + both(b, b0, b0 + n), [o], not start)

    def ps(bank, c0, c1, p0=0, p1=128, st=1):
        return reg("ps", 512 * bank + c0, 512 * bank + c1, p0, p1, st)

    def lanes(src):
        others = [c for c in T.cores if c != src]
        off = [c for c in others if topo.chip(c) != topo.chip(src)]
        on = [c for c in others if topo.chip(c) == topo.chip(src)]
        out = topo.engines(src, off[0])
        inn = [e for e in topo.engines(src, on[0]) if e not in out]
        m = {}
        for i, c in enumerate(off): m[c] = out[i * (len(out) // len(off)):(i + 1) * (len(out) // len(off))]
        for i, c in enumerate(on): m[c] = inn[i * (len(inn) // len(on)):(i + 1) * (len(inn) // len(on))]
        return m

    mine = lanes(core)
    sources = [T.cores[(rank + 1 + i) % 4] for i in range(3)]
    rest = [q for q in range(4) if q != rank]

    def slot(dst):
        return (rank - T.rank_of(dst) - 1) % 4

    def send(sem, pair, reads):
        def emit():
            tr = []
            for c in mine:
                rid, pid, _ = topo.addr(c)
                s, d = pair(c)
                tr.append(RemoteDMATransfer(dst_ids=[DstId(rid=rid, pnc=pid)], dma_engine_mask=sum(1 << e for e in mine[c]), remote_sem=T.sem[sem], src=s, dst=d))
                count["loc"] += len(mine[c])
            g.remote_dma_fused(tr, local_sem=T.sem.loc)
        calls.append(("send", "G", sem, reads, [], False, emit))

    incoming = sum(len(lanes(c)[core]) for c in sources)

    def cb(name, c0, c1):
        return T[name][:, c0:c1].bitcast(dt.uint8)

    def ship(sem, q, s0, n, dst, c0, c1):
        send(sem, lambda c: (cb(q, s0(c), s0(c) + n), cb("W", dst(c), dst(c) + n)), [reg(q, c0, c1)])
        send(sem, lambda c: (T[q + "s"][:, s0(c):s0(c) + n], T.Ws[:, dst(c):dst(c) + n]), [reg(q + "s", c0, c1)])

    def ti(i):
        return reg("ti", i, i + 1)

    def tf(i):
        return reg("tf", i, i + 1)

    def blk(name, c0, c1, a, n=1, st=1):
        return reg(name, c0, c1, 32 * a, 32 * (a + n), st)

    for h in range(2):
        for a in range(4):
            p0 = 32 * a + 16 * h
            if a % 2 == 0:
                dma("YS"[h], "d_nb", T.nbP[p0:p0 + 16, :], T.nb[:, 12 * a:12 * a + 24], [], [reg("nbP", 0, 24, p0, p0 + 16)])
            else:
                for k in range(2):
                    dma("YS"[h], "d_nb", T.nbP[p0:p0 + 16, 12 * k:12 * k + 12], T.nb[:, 12 * (a - k):12 * (a - k) + 12], [], [reg("nbP", 12 * k, 12 * k + 12, p0, p0 + 16)])
    for h in range(2):
        dma("Y", ("d_x", "d_y")[h], T.xt[:, 512 * h:512 * h + 512], T.x[:, 512 * h:512 * h + 512], [], [reg("xt", 512 * h, 512 * h + 512)])
    dma("S", "d_u", T.uz[:, 0:16], T.u[:, 0:16], [], [reg("uz", 0, 16)])
    dma("S", "d_v", T.uz[:, 16:32], T.v[:, 0:16], [], [reg("uz", 16, 32)])
    dma("Y", "d_bb", T.bt[:], T.bb[:], [], [reg("bt", 0, 1024)])
    dma("Y", "d_a", T.at[:], T.a[:], [], [reg("at", 0, 2048)])
    dma("Y", "d_w", T.wt[:], T.w[:], [], [reg("wt", 0, 512)])
    pI = ti(3)
    iota(pI, [[0, 1]], 0, 1)
    iota(reg("ID", 0, 256), [[1, 256]], 0)
    iota(reg("M16", 0, 80), [[0, 5], [1, 16]], 0)
    iota(reg("POS", 0, 96), [[16, 3], [0, 2], [1, 16]], 0)
    cut = min(rank + 1, 3)
    iota(reg("TAB", 0, 256 * cut), [[256, cut], [1, 2], [2, 128]], 256 * (3 - rank))
    iota(reg("TAB", 256 * cut, 1024), [[256, 4 - cut], [1, 2], [2, 128]], 0)
    for k, q in zip((1, 2, 3, 4), "VSVS"):
        n = min(256, WC - 256 * k)
        if q == "V":
            ts(reg("ID", 256 * k, 256 * k + n), reg("ID", 0, n), 256.0 * k, OP.add)
        else:
            act(reg("ID", 256 * k, 256 * k + n), reg("ID", 0, n), AF.Identity, bias=256.0 * k)
    for k in range(2):
        fill(reg("M", 512 * k, 512 * k + 512), 0.0)
    ts(ti(0), pI, 96, OP.bitwise_and)
    ts(ti(1), pI, 31, OP.bitwise_and)
    ts(ti(2), pI, 15, OP.bitwise_and)
    copy(reg("tf", 0, 4), reg("ti", 0, 4))
    act(tf(4), tf(0), AF.Identity, scale=7.0, bias=tf(3))
    act(reg("PJ", 0, 1), tf(0), AF.Identity, bias=tf(3))
    act(reg("PJ", 1, 2), reg("PJ", 0, 1), AF.Identity, bias=32.0)
    act(reg("PJ", 2, 3), reg("PJ", 0, 1), AF.Copy, scale=65536.0)
    act(tf(7), tf(2), AF.Sign, scale=-1.0, bias=15.0)
    act(tf(6), tf(7), AF.Copy, scale=BIG)
    ts(reg("LA2", 0, 65), reg("M16", 15, 80), tf(2), OP.is_equal, BIG, OP.mult)
    act(reg("LA1", 0, 64), reg("LA2", 1, 65), AF.Copy, scale=2.0)
    tt(reg("LM", 0, 64), reg("LA1", 0, 64), reg("LA2", 0, 64), OP.subtract)
    copy(reg("LM", 64, 128), reg("LM", 0, 64), "S")
    copy(reg("LM", 128, 256), reg("LM", 0, 128), "S")
    fill(reg("uz", 32, 512), 0.0)
    fill(reg("C1", 0, 32), TINY)
    fill(reg("H", 0, 512), 0.0)
    quant("PK0", 128, 256, "H")
    for a in range(4):
        fill(blk("PADD", 0, 1, a), float(FAR + LC * ((a - rank - 1) % 4 % 3) - 1))
    act(reg("GCOL", 0, 8), reg("ID", 0, 8), AF.Identity, scale=32.0, bias=tf(4))
    for i, q in enumerate(rest):
        act(blk("GCOL", 2 * i, 2 * i + 2, rank), blk("GCOL", 6, 8, rank), AF.Identity, bias=256.0 * (q - rank))
    fill(blk("PB", 192, 256, rank), 0.0)
    act(reg("IC", 0, 16), reg("ID", 0, 16), AF.Identity, scale=16.0, bias=tf(2))
    act(reg("ICS", 0, 8), reg("IC", 0, 8), AF.Identity, scale=-1.0, bias=-0.5)
    copy(reg("nbp", 0, 24), reg("nbP", 0, 24))
    gather(reg("FR", 0, 192), reg("ID", 0, 1024), reg("nbp", 0, 12))
    gather(reg("FR", 192, 384), reg("ID", 0, 1024), reg("nbp", 12, 24), "S")
    copy(reg("FA", 0, 128), reg("FR", 2, 384, st=3))
    copy(blk("FA", 128, 256, 0, 2), blk("FA", 0, 128, 2, 2))
    copy(blk("FA", 128, 256, 2, 2), blk("FA", 0, 128, 0, 2))
    for h in range(2):
        quant("Q0", 128 * h, 128 * h + 128, "xt", 512 * h)
    quant("UV1", 0, 128, "uz")
    for c in range(2):
        mm(c, "Q0", 128 * c, "UV1", 0, 128)
    copy(reg("ec", 0, 2), ps(0, 0, 513, st=512), "S")
    send("r_e", lambda c: (T.ec[:, 0:2], T.eld[slot(c)]), [reg("ec", 0, 2)])
    arrive("r_e", incoming, reg("eld", 0, 3))
    for k in range(2):
        fill(reg("UL", 8 * k, 8 * k + 8), 4 * k)
        pick("UV2", 128 * k, 128 * k + 128, "UV1", 0, 128, reg("UL", 8 * k, 8 * k + 8))
    dma("Y", "d_q", cb("W", 0, 256), cb("Q0", 0, 256), [reg("Q0", 0, 256)], [reg("W", 0, 256)])
    dma("Y", "d_q", T.Ws[:, 0:256], T.Q0s[:, 0:256], [reg("Q0s", 0, 256)], [reg("Ws", 0, 256)])
    for c in range(6):
        ts(reg("EQ", 256 * c, 256 * c + 256), reg("FA", 0, 256), reg("GCOL", c, c + 1), OP.is_equal)
        scan(reg("SC", 128 * c, 128 * c + 128), reg("EQ", 256 * c, 256 * c + 128), reg("EQ", 256 * c + 128, 256 * c + 256))
        act(reg("PB", 32 * c, 32 * c + 32), reg("H", 192, 224), AF.Sign, bias=reg("SC", 128 * c + 127, 128 * c + 128))
        o = 192 + 32 * (c % 2)
        act(blk("PB", o, o + 32, rest[c // 2]), blk("H", 192, 224, rank), AF.Sign, bias=blk("SC", 128 * c + 127, 128 * c + 128, rank))
    turn(reg("PR", 0, 256), reg("PB", 0, 256))
    scan(reg("SCN", 0, 256), reg("PR", 0, 256), reg("PR", 0, 256), OP.max)
    nv = 6 - LEN_S
    for c in range(nv):
        ts(reg("LE", 256 * c, 256 * c + 256), reg("SCN", 0, 256), reg("IC", c, c + 1), OP.is_le)
        scan(reg("LC2", 128 * c, 128 * c + 128), reg("LE", 256 * c, 256 * c + 128), reg("LE", 256 * c + 128, 256 * c + 256))
    for c in range(nv, 6):
        act(reg("LJ", 256 * (c % 3), 256 * (c % 3) + 255), reg("SCN", 0, 255), AF.Sign, bias=reg("ICS", c, c + 1), accum=reg("LS", c, c + 1))
    ts(reg("LST", 0, nv), reg("LC2", 127, 128 * nv, st=128), 255.0, OP.min)
    ts(reg("LST", nv, 6), reg("LS", nv, 6), -0.5, OP.mult, 127.5, OP.add)
    send("r_l", lambda c: (T.LST[:, 0:6], T.LA[:, 6 * slot(c):6 * slot(c) + 6]), [reg("LST", 0, 6)])
    arrive("r_l", incoming, reg("LA", 0, 18))
    act(reg("SLf", 0, 256), reg("SCN", 0, 256), AF.Identity, bias=reg("PADD", 0, 1))
    for q in rest:
        dma("Y", "d_m", T.M[0:128:16, 256 * q:256 * q + 256], T.SLf[32 * q:32 * q + 8, :], [blk("SLf", 0, 256, q)], [reg("M", 256 * q, 256 * q + 256)])
    for k in range(3):
        latch(reg("LQ", 64 * k, 64 * k + 64), reg("FR", k, 192, st=3), 64)
    ts(reg("nbK", 0, 8), reg("LQ", 15, 128, st=16), tf(6), OP.add, float(-256 * rank), OP.add)
    ts(reg("nbK", 8, 12), reg("LQ", 143, 192, st=16), tf(6), OP.add)
    for h in range(2):
        ts(reg("nbD", h, 8, st=2), reg("LQ", 143, 192, st=16), tf(6), OP.add)
    gather(reg("TG", 0, 64), reg("TAB", 0, 1024), reg("nbK", 8, 12), "S")
    latch(reg("LQ", 192, 256), reg("TG", 0, 64), 64)
    ts(reg("nbe", 0, 4), reg("LQ", 207, 256, st=16), tf(6), OP.add)
    for d in range(4):
        dma("Y", "d_e", T.TAB[32 * d:32 * d + 1, 0:768], T.eld[0:3], [reg("eld", 0, 3)], [reg("TAB", 0, 768, 32 * d, 32 * d + 1)])
    quant("Qb", 0, 256, "bt")
    mm(5, "UV2", 0, "Q0", 0, 256)
    mm(4, "UV2", 128, "Qb", 0, 256)
    ts(reg("Ft", 0, 32), reg("ID", 0, 32), tf(1), OP.is_lt, 2.0 ** -24, OP.mult)
    copy(reg("E1", 0, 256), ps(5, 0, 256), "S")
    for a in range(4):
        copy(blk("fb", 0, 64, a), ps(4, 64 * a, 64 * a + 64, 32 * a, 32 * a + 32), "S")
    for b in range(2):
        act(reg("Fm", 32 * b, 32 * b + 32), reg("Ft", 0, 32), AF.Identity, bias=PRED)
    copy(reg("Mo", 0, 256), reg("ID", 0, 256), "S")
    for k in range(2):
        ts(reg("FN", k, 256, st=2), reg("FR", k, 384, st=3), float(-256 * rank), OP.add)
    copy(blk("FN", 256, 512, 0), blk("FN", 0, 256, 2))
    for h in range(2):
        dma("Y", "d_g", T.nbG[64 * h:64 * h + 64, 0:32], T.FN[0:32:8, 0:512], [blk("FN", 0, 512, 0)], [reg("nbG", 0, 32, 64 * h, 64 * h + 64)])
    for h in range(2):
        dma("Y", "d_h", T.nbG[64 * h:64 * h + 64, 32:48], T.FA[0:32:8, 0:256], [blk("FA", 0, 256, 0)], [reg("nbG", 32, 48, 64 * h, 64 * h + 64)])
    for t in range(4):
        copy(reg("bbT", 256 * t, 256 * t + 256), reg("bt", t, 1024, st=4), "S")
    for d in rest:
        copy(blk("LA", 0, 18, d), blk("LA", 0, 18, rank))
    pick("SND", 0, 288, "Q0", 0, 256, reg("LA", 0, 18))
    ship("r_c", "SND", lambda c: LC * sources.index(c), LC, lambda c: FAR + LC * slot(c), 0, 3 * LC)
    arrive("r_c", 2 * incoming, *both("W", FAR, FAR + 3 * LC))

    z0, z1, z2, EG, zr = reg("z0", 0, 64), reg("z1", 0, 64), reg("z2", 0, 64), reg("EG", 0, 64), reg("Zc", 256, 320)
    M = reg("M", 0, 1024)
    Mo = reg("Mo", 0, 256)
    C005 = 13421773.0 * 2.0 ** -28

    def at_places(oh, th, xh, o, pay):
        for b in range(2):
            ts(reg(oh, o + 96 * b, o + 96 * b + 96), reg("POS", 0, 96), reg("RS", 128 * b + 127, 128 * b + 128), OP.is_equal, pay[b], OP.mult)
            turn(reg(th, o + b, o + 192, st=2), reg(oh, o + 96 * b, o + 96 * b + 96))
        for c in range(o, o + 192, 64):
            scan(blk(xh, c, c + 64, 0, 2), blk(th, c, c + 64, 0, 2), blk(th, c, c + 64, 2, 2))

    def joined(out, c0, xh, o):
        for d in range(2):
            tt(blk(out, c0, c0 + 3, d), blk(xh, o + 63, o + 192, 0, st=64), blk(xh, o + 63, o + 192, 1, st=64), OP.add)

    def to_list(out, c0, src, s0, n):
        for d in (0, 2):
            copy(blk(out, c0, c0 + n, d, 2), blk(src, s0, s0 + n, 0, 2))

    quant("Qa", 0, 256, "at")
    quant("Qa", 256, 512, "at", 1024)
    quant("Qw", 0, 128, "wt")
    mm(5, "Qw", 0, "Q0", 0, 256)
    copy(reg("ys", 0, 256), ps(5, 0, 256), "S")
    for t in range(R):
        SL, SR = "SL%d" % t, "SR%d" % t
        J = reg("J", 4 * t, 4 * t + 3)
        wend, w0 = WEND[t], OWN[t]
        if t == 0:
            gather(EG, reg("E1", 0, 256), reg("nbK", 0, 4), "S")
            tt_by(z0, reg("E1", 0, 256), reg("nbK", 4, 8), EG, OP.add)
            tt_by(z1, reg("TAB", 0, 768), reg("nbe", 0, 4), z0, OP.add)
            for b in range(2):
                act(reg("zK", 32 * b, 32 * b + 32), reg("FR", 1 + 96 * b, 96 * b + 96, st=3), AF.Identity, scale=256.0, bias=65536.0 * 32 * b - 257.0 * 256 * rank)
            tt(reg("PAB", 0, 64), reg("zK", 0, 64), reg("FR", 0, 192, st=3), OP.add)
            turn(reg("PAYT", 0, 64), reg("PAB", 0, 64))
            ts(reg("PAY", 0, 2), reg("PAYT", 0, 64, st=32), reg("PJ", 2, 3), OP.add)
            act(reg("PC", 0, 64), M, AF.Identity, bias=float(-FAR), by=reg("nbK", 8, 12))
            turn(reg("PAYT", 64, 128), reg("PC", 0, 64))
        else:
            a0 = ARR[t - 1]
            mm(6, "UV2", 0, "W", a0, 3 * K)
            copy(reg("E1", a0, a0 + 3 * K), ps(6, 0, 3 * K))
            tt_by(z1, reg("E1", FAR, wend), reg("EO", 0, 4), z0, OP.add)
        tt(z2, z1, reg("fb", 0, 64), OP.subtract)
        if t == 0:
            turn(reg("zB", 0, 64), z2)
            for b in range(2):
                act(reg("ZT", 32 * b, 32 * b + 32), reg("C1", 0, 32), AF.Abs, bias=reg("zB", 32 * b, 32 * b + 1))
            turn(zr, reg("ZT", 0, 64))
        else:
            act(zr, z2, AF.Abs, bias=TINY)
            turn(reg("ZT", 0, 64), zr)
        tt(reg("Zc", 192, 256), zr, reg("Fm", 0, 64), OP.mult)
        moves = [(0, 2, 2, 0), (2, 0, 2, 0), (0, 1, 1, 1), (1, 0, 1, 1), (2, 3, 1, 1), (3, 2, 1, 1), (0, 3, 1, 2), (2, 1, 1, 2), (3, 0, 1, 2), (1, 2, 1, 2)]
        for n, (d, s, w, x) in enumerate(moves):
            o = blk("Zc", 64 * x, 64 * x + 64, d, w)
            f = PRED if s > d else 1.0
            if n < len(moves) - VX:
                if t == 0:
                    act(o, blk("Zc", 256, 320, s, w), AF.Copy, scale=f)
                else:
                    act(o, blk("z2", 0, 64, s, w), AF.Abs, scale=f, bias=TINY * f)
            elif s > d:
                ts(o, blk("Zc", 256, 320, s, w), f, OP.mult)
            else:
                copy(o, blk("Zc", 256, 320, s, w))
        ts(reg("MK", 224, 256), reg("Zc", 288, 320), reg("ZT", 0, 1), OP.is_gt)
        ts(reg("MK", 448, 512), reg("Zc", 224, 288), reg("ZT", 32, 33), OP.is_ge)
        for b in range(2):
            n = 224 - 32 * b
            ts(reg("MK", 256 * b, 256 * b + n), reg("Zc", 0, n), reg("ZT", 32 * b, 32 * b + 1), OP.is_ge)
            scan(reg("RS", 128 * b, 128 * b + 128), reg("MK", 256 * b, 256 * b + 128), reg("MK", 256 * b + 128, 256 * b + 256))
        if t == 0:
            at_places("OF", "TF", "XF", 0, [reg("PAY", b, b + 1) for b in range(2)])
            joined("Ri", 0, "XF", 0)
            ts(blk("Di", 0, 3, 0, 2), blk("Ri", 0, 3, 0, 2), 255, OP.bitwise_and)
            ts(blk("Di", 3, 6, 0, 2), blk("Ri", 0, 3, 0, 2), 8, OP.logical_shift_right, 255, OP.bitwise_and)
            ts(blk("Di", 6, 9, 0, 2), blk("Ri", 0, 3, 0, 2), 16, OP.logical_shift_right)
            to_list("PO", 0, "Di", 0, 9)
            J = reg("PO", 6, 9)
            copy(blk("YJ", 0, 3, 0), blk("Di", 6, 9, 0))
            pick("PK0", K, 3 * K, "Q0", 0, 256, reg("PO", 0, 6))
            at_places("OF", "TF", "XF", 192, [reg("PAYT", 64 + 32 * b, 65 + 32 * b) for b in range(2)])
            joined("Ri", 3, "XF", 192)
            to_list("PF", 0, "Ri", 3, 3)
            pick("PK0", 0, K, "W", FAR, wend, reg("PF", 0, 3))
        else:
            at_places("OH", "TH", "XH", 0, [reg("PJ", b, b + 1) for b in range(2)])
            joined("YJ", 3 * t, "XH", 0)
            to_list("J", 4 * t, "YJ", 3 * t, 3)
        if t < 2:
            ts(reg(SL, 0, 3), J, float(256 * rank), OP.add)
            send("r_s%d" % t, lambda c, SL=SL, SR=SR: (T[SL][:, 0:3], T[SR][:, 3 * slot(c):3 * slot(c) + 3]), [reg(SL, 0, 3)])
            arrive("r_s%d" % t, incoming, reg(SR, 0, 9))
        scatter(Mo, J, reg("ID", w0, w0 + K))
        if t == 2:
            latch(reg("FT", 0, 256), Mo, 256)
            ts(reg("FO", 0, 16), reg("FT", 15, 256, st=16), tf(6), OP.add)
        for b in range(4):
            gather(reg("G4", K * b, K * b + K), reg("bbT", 256 * b, 256 * b + 256), J, "S")
        if t == 0:
            for k in range(3):
                for b in range(4):
                    mm(b, "Qa", 128 * b, "PK0", K * ((k + 1) % 3), 128, k == 0, k == 2)
            for b in range(4):
                act(reg("SU", K * b, K * b + K), ps(b, 0, K), AF.Copy, scale=C005)
                tt(reg("H", b, 4 * K, st=4), reg("SU", K * b, K * b + K), reg("G4", K * b, K * b + K), OP.add)
            mm(7, "UV2", 0, "W", FAR, 3 * LC)
            copy(reg("E1", FAR, FAR + 3 * LC), ps(7, 0, 3 * LC), "S")
        else:
            for b in range(4):
                tt_by(reg("H", b, 4 * K, st=4), reg("ST", 256 * b, 256 * b + 256), J, reg("G4", K * b, K * b + K), OP.add)
        quant("W", w0, w0 + 128, "H")
        if t < 2:
            ship("r_n%d" % t, "W", lambda c, w0=w0: w0, K, lambda c, t=t: ARR[t] + K * slot(c), w0, w0 + K)
            arrive("r_n%d" % t, 2 * incoming, *both("W", ARR[t], ARR[t] + 3 * K))
            u = t + 1
            PA = "PA%d" % u
            mm(7, "UV2", 0, "W", w0, 128)
            copy(reg("en", K * t, K * t + K), ps(7, 0, K), "S")
            scatter(reg("E1", 0, 256), J, reg("en", K * t, K * t + K))
            gather(EG, reg("E1", 0, 256), reg("nbK", 0, 4), "S")
            tt_by(z0, reg("E1", 0, 256), reg("nbK", 4, 8), EG, OP.add)
            for k in range(2):
                gather(reg("LRo", 256 * k, 256 * k + 256), Mo, reg("nbG", 16 * k, 16 * k + 16), "S")
            dma("Y", "d_l%d" % (2 * t), T.LIo[:, 32 * t:32 * t + 32], T.LRo[0:128:16, 0:512], [reg("LRo", 0, 512)], [reg("LIo", 32 * t, 32 * t + 32)])
            copy(reg("Lu", 48 * t, 48 * t + 32), reg("LIo", 32 * t, 32 * t + 32))
            for k in range(2):
                o = 48 * t + 16 * k
                pick(PA, 256 * k, 256 * k + 256, "W", 0, w0 + K, reg("Lu", o, o + 16))
                for b in range(4):
                    mm(b, "Qa", 128 * b, PA, 256 * k, 256, k == 0, False)
            scatter(M, reg(SR, 0, 9), reg("ID", ARR[t], ARR[t] + 3 * K))
            gather(reg("PD", 0, 128), M, reg("nbD", 0, 8), "S")
            turn(reg("PT", 0, 128), reg("PD", 0, 128))
            ts(reg("EO", 0, 4), reg("PT", 0, 128, st=32), float(-FAR), OP.add)
            gather(reg("LRf", 0, 256), M, reg("nbG", 32, 48), "S")
            dma("Y", "d_l%d" % (2 * t + 1), T.LIf[:, 16 * t:16 * t + 16], T.LRf[0:128:16, 0:256], [reg("LRf", 0, 256)], [reg("LIf", 16 * t, 16 * t + 16)])
            o = 48 * t + 32
            ts(reg("Lu", o, o + 16), reg("LIf", 16 * t, 16 * t + 16), float(-FAR), OP.add)
            pick(PA, 512, 768, "W", FAR, WEND[u], reg("Lu", o, o + 16))
            for b in range(4):
                mm(b, "Qa", 128 * b, PA, 512, 256, False, True)
            for b in range(4):
                act(reg("ST", 256 * b, 256 * b + 256), ps(b, 0, 256), AF.Copy, scale=C005)
        else:
            for h in range(2):
                pick("FIN", 128 * h, 128 * h + 128, "W", 0, WC, reg("FO", 8 * h, 8 * h + 8))
        for c in range(3):
            dma("Y", "d_nd", T.nd[t:t + 1, 16 * c:16 * c + 16], T.YJ[0:16, 3 * t + c:3 * t + c + 1], [blk("YJ", 3 * t, 3 * t + 3, 0)], [])
        mm(4, "Qw", 0, "W", w0, 128)
        copy(reg("yn", K * t, K * t + K), ps(4, 0, K), "S")
        scatter(reg("ys", 0, 256), J, reg("yn", K * t, K * t + K))

    dma("Y", "d_out", T.oc[:, 0:1024], cb("FIN", 0, 256), [reg("FIN", 0, 256)], [])
    for k in range(4):
        dma("YYSS"[k], "d_out", T.osc[4 * k:4 * k + 4, 0:256], T.FINs[32 * k:32 * k + 4, 0:256], [reg("FINs", 0, 256)], [])
    dma("S", "d_out", T.y[:], T.ys[:], [reg("ys", 0, 256)], [])
    for i in ORDER or range(len(calls)):
        issue(*calls[i])
    for s in ("v", "s", "p", "gq", "d_q", "d_g", "d_h", "d_nd", "d_out", "loc"):
        if know["G"].get(s, 0) < count[s]:
            g.wait_ge(T.sem[s], count[s])
